import numpy as np, ml_dtypes
CORES = [16,18,20,22]
N = 4
BF = ml_dtypes.bfloat16
def gentries(a):
    return np.ascontiguousarray(a.reshape(8, 16, -1).transpose(0, 2, 1)).reshape(8, -1)
def gtable(e):
    e = np.asarray(e); return np.ascontiguousarray(e.reshape(8, -1, 16).transpose(0, 2, 1)).reshape(128, -1).astype(np.int32)
C, CAP, P, H = 1024, 384, 8192, 3
def walk(cells, first, pads):
    x = cells.astype(np.float32).astype(np.int32).reshape(N, 8, 16, C); p = pads.astype(np.float32).astype(np.int32).reshape(N, 8, 16, P)
    keys = [gentries(a) for a in first]; most = 0; sent = {}
    now = {(r, g): (x[r, g], keys[r][g]) for r in range(N) for g in range(8)}
    for h in range(H):
        sent = {}
        for r in range(N):
            for g in range(8):
                v, key = now[r, g]; v = (v - p[r, g][:, key]) & 255
                to = v[0] & (N - 1); key = v[1] + 256 * (v[2] & (P // 256 - 1))
                for q in range(N):
                    m = to == q; sent[r, q, g] = (v[:, m], key[m]); most = max(most, int(np.count_nonzero(m)))
        now = {(q, g): (np.concatenate([sent[r, q, g][0] for r in range(N)], axis=1), np.concatenate([sent[r, q, g][1] for r in range(N)])) for q in range(N) for g in range(8)}
    return sent, most
def parts(rng, n, w, t=-1):
    w = np.array(w, np.float64); k = 0
    if t >= 0:
        w[t] = 0; k = min(n, CAP)
    a = np.add.accumulate(w); i = np.searchsorted(a, rng.random(n - k) * a[-1], side="right")
    c = np.minimum(np.bincount(np.minimum(i, N - 1), minlength=N), CAP)
    if t >= 0: c[t] = k
    o = rng.permutation(N); o = o[np.argsort(w[o] == 0, kind="stable")]
    for r in o: c[r] += min(n - int(np.sum(c)), CAP - int(c[r]))
    return c
def routes(rng, count, runs=False):
    to = np.zeros((8, N, C, H), np.int64)
    for g in range(8):
        at = np.repeat(np.arange(N), C); t = to[g].reshape(N * C, H)
        for h in range(H):
            new = at.copy()
            for q in range(N):
                i = np.nonzero(at == q)[0]; d = np.repeat(np.arange(N), count(h, g, q, len(i)))
                new[i] = d if runs and g % 2 == 0 else rng.permutation(d)
            t[:, h] = new; at = new
    return to
def dress(to, first, p, body, u):
    x = body.copy()
    for g in range(8):
        for r in range(N):
            key = np.arange(P); at = np.full(P, r); v = np.stack([at, key & 255, key >> 8]); code = np.zeros(P, np.int64)
            for h in range(1, H):
                v = (v - np.stack([p[at, g, s, key] for s in range(3)])) & 255
                at = v[0] & (N - 1); key = v[1] + 256 * (v[2] & (P // 256 - 1)); code = code * N + at
            order = np.argsort(code, kind="stable"); a = np.searchsorted(code[order], np.arange(N ** (H - 1))); b = np.searchsorted(code[order], np.arange(N ** (H - 1)), side="right")
            q, i = np.nonzero(to[g, :, :, 0] == r); c = np.zeros(len(q), np.int64)
            for h in range(1, H): c = c * N + to[g, q, i, h]
            k = order[a[c] + np.floor(u[q, g, i] * (b - a)[c]).astype(np.int64)]
            x[q, g, 0, i] = x[q, g, 0, i] // N * N + r
            x[q, g, 1, i] = k & 255
            x[q, g, 2, i] = x[q, g, 2, i] // (P // 256) * (P // 256) + (k >> 8)
    x = (x + np.take_along_axis(p, first[:, :, None, :], axis=3)) & 255
    return {"cells": x.reshape(N, 128, C).astype(np.float32).astype(BF), "first": np.stack([gtable(e) for e in first]), "pads": p.reshape(N, 128, P).astype(np.float32).astype(BF)}
def setup_inputs(rng):
    w = 1 + rng.random((H, 8, N, N)); to = routes(rng, lambda h, g, q, n: parts(rng, n, w[h, g, q]))
    return dress(to, rng.integers(0, P, (N, 8, C)), rng.integers(0, 256, (N, 8, 16, P)), rng.integers(0, 256, (N, 8, 16, C)), rng.random((N, 8, C)))
def setup_inputs_ends(rng):
    w = 1 + rng.random((H, 8, N, N)); to = routes(rng, lambda h, g, q, n: parts(rng, n, w[h, g, q]))
    p = rng.integers(0, 256, (N, 8, 16, P)); p[0, :, :, 0] = 0
    full = rng.integers(0, 2, (N, 8, C)); body = rng.integers(0, 256, (N, 8, 16, C)) * full[:, :, None, :]
    u = rng.integers(0, 2, (N, 8, C)) * (1 - 2.0 ** -20)
    assert ((to == 0).all(axis=3).transpose(1, 0, 2) & (full == 0) & (u == 0)).any()
    return dress(to, rng.integers(0, 2, (N, 8, C)) * (P - 1), p, body, u)
def setup_inputs_full(rng):
    t = rng.integers(0, N, (H, 8)); to = routes(rng, lambda h, g, q, n: parts(rng, n, np.ones(N), int(t[h, g])), True)
    return dress(to, rng.integers(0, P, (N, 8, C)), rng.integers(0, 256, (N, 8, 16, P)), rng.integers(0, 256, (N, 8, 16, C)), rng.random((N, 8, C)))
def setup_inputs_bare(rng):
    s = rng.integers(0, N, H)
    def count(h, g, q, n):
        w = np.ones(N); none = (g % 2 == 0 and h == 0) or (g % 2 == 1 and h == H - 1)
        w[(g // 2 + s[h]) % N if none else (q + g + s[h]) % N] = 0
        return parts(rng, n, w)
    to = routes(rng, count)
    return dress(to, rng.integers(0, P, (N, 8, C)), rng.integers(0, 256, (N, 8, 16, P)), rng.integers(0, 256, (N, 8, 16, C)), rng.random((N, 8, C)))
def setup_inputs_spread(rng):
    w = np.exp2(rng.integers(-4, 5, (H, 8, N, N))); to = routes(rng, lambda h, g, q, n: parts(rng, n, w[h, g, q]))
    def skew(k):
        return np.minimum(np.floor(256 * rng.random((N, 8, 16, k)) ** np.exp2(rng.integers(-3, 4, (N, 8, 16, 1)))), 255).astype(np.int64)
    p = skew(P); p[:, :, :3] = rng.integers(0, 256, (N, 8, 3, P))
    return dress(to, rng.integers(0, P, (N, 8, C)), p, skew(C), rng.random((N, 8, C)))
def check_inputs(d):
    bad = []
    for a in ("cells", "pads"):
        v = d[a].astype(np.float32)
        if not ((v >= 0) & (v <= 255) & (v == np.floor(v))).all(): bad.append(a)
    if not ((d["first"] >= 0) & (d["first"] < P)).all(): bad.append("first")
    if not bad and walk(d["cells"], d["first"], d["pads"])[1] > CAP: bad.append("places")
    return bad
def reference(cells, first, pads):
    sent, most = walk(cells, first, pads); y = np.zeros((N, 8, 16, N * CAP), np.float32)
    for r in range(N):
        for q in range(N):
            for g in range(8):
                v = sent[q, r, g][0][:, :CAP]; y[r, g, :, q * CAP:q * CAP + v.shape[1]] = v
    return {"y": y.reshape(N, 128, N * CAP)}

@@ -1,0 +1,343 @@
+from concourse.bass import DstId, RemoteDMATransfer
+from concourse.mybir import AluOpType as A, ActivationFunctionType as F
+
+N, C, CAP, P, H = 4, 1024, 384, 8192, 3
+S = N * CAP
+DUMP = 512
+BIG = 2048
+EMPTY = -1024
+KB = CAP // 16
+
+bf, f16, f32, i32, u16 = "bfloat16", "float16", "float32", "int32", "uint16"
+SCRATCH = {
+    "pad": ("sbuf", [128, P], bf), "cel": ("sbuf", [128, C], bf), "fi": ("sbuf", [128, 64], i32),
+    "cp": ("sbuf", [128, 512], bf),
+    "X": ("sbuf", [128, 144], f32), "Xg": ("sbuf", [128, 128], f32), "Dio": ("sbuf", [128, 128], f32),
+    "pk": ("sbuf", [128, 1], i32), "gsi": ("sbuf", [128, 1], i32),
+    "kf": ("sbuf", [128, 1], f32), "gs": ("sbuf", [128, 1], f32), "sf": ("sbuf", [128, 1], f32),
+    "c15": ("sbuf", [128, 1], f32), "w0": ("sbuf", [128, 1], f32), "wa": ("sbuf", [128, 1], f32),
+    "wb": ("sbuf", [128, 1], f32), "wk": ("sbuf", [128, 1], f32),
+    "W0": ("sbuf", [128, 144], bf), "W1": ("sbuf", [128, 144], bf), "Wk": ("sbuf", [128, 144], bf),
+    "I": ("sbuf", [128, 128], bf), "I16": ("sbuf", [128, 16], bf), "Z": ("sbuf", [128, 128], bf),
+    "BO": ("sbuf", [128, 128], f16), "ta": ("sbuf", [128, 128], f16), "tc": ("sbuf", [128, 128], f16),
+    "td": ("sbuf", [128, 128], f16), "L": ("sbuf", [128, 128], f16), "U": ("sbuf", [128, 128], f16),
+    "m5": ("sbuf", [128, 480], bf), "P5": ("sbuf", [128, 480], f16), "M5": ("sbuf", [128, 480], f16),
+    "E": ("sbuf", [128, 384], f16),
+    "li": ("sbuf", [128, 96], i32), "la": ("sbuf", [128, 96], i32), "lb": ("sbuf", [128, 96], i32),
+    "ku": ("sbuf", [128, 96], u16), "lu": ("sbuf", [128, 64], u16), "hu": ("sbuf", [128, 64], u16),
+    "pu": ("sbuf", [128, 96], u16),
+    "G": ("sbuf", [128, C], bf), "Sel": ("sbuf", [128, C], bf),
+    "n": ("sbuf", [128, S], bf), "t": ("sbuf", [128, S], bf), "d": ("sbuf", [128, S], bf), "sg": ("sbuf", [128, S], bf),
+    "yf": ("sbuf", [128, S], f32),
+    "psK": ("psum", [128, 512], f32), "psD": ("psum", [128, 512], f32),
+    "psA": ("psum", [128, 512], f32), "psB": ("psum", [128, 512], f32),
+}
+for _h in range(H):
+    SCRATCH["win%d" % _h] = ("sbuf", [128, DUMP + S], bf)
+    SCRATCH["R%d" % _h] = ("sbuf", [128, S], bf)
+for _q in range(N):
+    SCRATCH["psP%d" % _q] = ("psum", [128, 512], f32)
+
+SEMAPHORES = (["cv", "ca", "cp", "cg", "dfi", "dcp", "dcel", "dpad", "ar0", "ar1", "ls0", "ls1", "ls2"]
+              + ["al%d" % q for q in range(N)] + ["st%d" % q for q in range(N)])
+
+
+def rank_program(g, core, T, topo):
+    rank = T.rank_of(core)
+    if rank is None:
+        return
+    Q = {"v": g.vector, "a": g.scalar, "p": g.tensor, "g": g, "s": g.sync}
+    OWN = {"v": "cv", "a": "ca", "p": "cp", "g": "cg"}
+    known = {q: {} for q in Q}
+    count = {}
+    waited = {}
+    log = []
+
+    def need(q, tok):
+        sem, val, clock = tok
+        if known[q].get(sem, 0) < val:
+            Q[q].wait_ge(T.sem[sem], val)
+            waited[sem] = max(waited.get(sem, 0), val)
+        for s_, v_ in list(clock.items()) + [(sem, val)]:
+            if known[q].get(s_, 0) < v_:
+                known[q][s_] = v_
+
+    def op(q, fn, r=(), w=(), sem=None, inc=1, after=()):
+        eng = q if sem is None else "dma"
+        toks = list(after)
+        for acc, wr in [(x, False) for x in r] + [(x, True) for x in w]:
+            for (b, lo, hi, owr, oq, tok) in log:
+                if b != acc[0] or hi <= acc[1] or acc[2] <= lo:
+                    continue
+                same = oq == eng and eng != "dma"
+                if same and q == "p":
+                    continue
+                if wr or owr or (b.startswith("ps") and not same):
+                    toks.append(tok)
+        best = {}
+        for tok in toks:
+            if tok[0] not in best or best[tok[0]][1] < tok[1]:
+                best[tok[0]] = tok
+        for tok in sorted(best.values(), key=lambda k: -len(k[2])):
+            need(q, tok)
+        ins = fn()
+        s_ = OWN[q] if sem is None else sem
+        count[s_] = count.get(s_, 0) + inc
+        ins.then_inc(T.sem[s_], inc)
+        tok = (s_, count[s_], dict(known[q]))
+        for acc, wr in [(x, False) for x in r] + [(x, True) for x in w]:
+            log.append((acc[0], acc[1], acc[2], wr, eng, tok))
+        return tok
+
+    def al(b):
+        return (b, 0, 1 << 20)
+
+    V, ACT, PE = g.vector, g.scalar, g.tensor
+
+    def ts(out, in0, s1, s2, o0, o1, r, w):
+        if o1 is None:
+            return op("v", lambda: V.tensor_scalar(out, in0, s1, None, o0), r, w)
+        return op("v", lambda: V.tensor_scalar(out, in0, s1, s2, o0, o1), r, w)
+
+    def tt(out, in0, in1, o, r, w):
+        return op("v", lambda: V.tensor_tensor(out, in0, in1, o), r, w)
+
+    def cpy(out, in_, r, w):
+        return op("v", lambda: V.tensor_copy(out, in_), r, w)
+
+    def act(out, in_, func, bias, scale, r, w):
+        return op("a", lambda: ACT.activation(out, in_, func, bias=bias, scale=scale), r, w)
+
+    def iota(out, pattern, base, cm, w, flag=True):
+        if flag:
+            return op("g", lambda: g.iota(out, pattern, base, cm, allow_small_or_imprecise_dtypes=True), (), w)
+        return op("g", lambda: g.iota(out, pattern, base, cm), (), w)
+
+    def mm(calls, r, w, after=()):
+        def run():
+            ins = None
+            for (o, l, x, st, sp) in calls:
+                ins = PE.matmul(o, l, x, st, sp)
+            return ins
+        return op("p", run, r, w, after=after)
+
+    def to_list(ps, c0, W, src, lo, hi, start, stop):
+        k = (hi - lo) // 16
+        return [(T[ps][:, c0:c0 + k], T[W][:, 15 - r:143 - r], T[src][:, lo + r:hi:16], start and r == 0, stop and r == 15)
+                for r in range(16)]
+
+    op("s", lambda: g.sync.dma_start(T.fi[:], T.first[:]), (), [al("fi")], sem="dfi", inc=16)
+    op("a", lambda: g.scalar.dma_start(T.cel[:], T.cells[:]), (), [al("cel")], sem="dcel", inc=16)
+    op("s", lambda: g.sync.dma_start(T.cp[:], T.pads[0:128:16, :]), (), [al("cp")], sem="dcp", inc=16)
+    op("s", lambda: g.sync.dma_start(T.pad[:], T.pads[:]), (), [al("pad")], sem="dpad", inc=16)
+
+    iota(T.pk[:], [[0, 1]], 0, 1, [al("pk")], False)
+    iota(T.kf[:], [[0, 1]], 0, 1, [al("kf")])
+    iota(T.X[:], [[1, 144]], 0, 0, [al("X")])
+    iota(T.Xg[:], [[16, 8], [0, 16]], 0, 0, [al("Xg")])
+    iota(T.Dio[:], [[0, 4], [16, 32]], 0, 1, [al("Dio")])
+    iota(T.m5[:], [[0, 96], [4096, 5]], 0, 0, [al("m5")])
+    iota(T.win0[:, DUMP:], [[0, S]], EMPTY, 0, [al("win0")])
+    iota(T.win1[:, DUMP:], [[0, S]], EMPTY, 0, [al("win1")])
+
+    op("v", lambda: V.memset(T.Z[:], 0.0), (), [al("Z")])
+    ts(T.gsi[:], T.pk[:], 112, None, A.bitwise_and, None, [al("pk")], [al("gsi")])
+    cpy(T.gs[:], T.gsi[:], [al("gsi")], [al("gs")])
+    ts(T.sf[:], T.kf[:], T.gs[:], None, A.subtract, None, [al("kf"), al("gs")], [al("sf")])
+    ts(T.c15[:], T.gs[:], 15.0, None, A.add, None, [al("gs")], [al("c15")])
+    ts(T.w0[:], T.sf[:], 0.0, None, A.is_equal, None, [al("sf")], [al("w0")])
+    ts(T.I16[:], T.X[:, 0:16], T.sf[:], None, A.is_equal, None, [al("X"), al("sf")], [al("I16")])
+    ts(T.W1[:], T.X[:], T.c15[:], -1.0, A.is_equal, A.mult, [al("X"), al("c15")], [al("W1")])
+    ts(T.W0[:], T.X[:], T.c15[:], T.w0[:], A.is_equal, A.mult, [al("X"), al("c15"), al("w0")], [al("W0")])
+    ts(T.I[:], T.X[:, 0:128], T.kf[:], None, A.is_equal, None, [al("X"), al("kf")], [al("I")])
+
+    ts(T.la[:, 0:64], T.fi[:], 511, None, A.bitwise_and, None, [al("fi")], [al("la")])
+    ts(T.lb[:, 0:64], T.fi[:], 9, None, A.logical_shift_right, None, [al("fi")], [al("lb")])
+    cpy(T.lu[:], T.la[:, 0:64], [al("la")], [al("lu")])
+    cpy(T.hu[:], T.lb[:, 0:64], [al("lb")], [al("hu")])
+    cpy(T.ku[:, 0:64], T.fi[:], [al("fi")], [al("ku")])
+    for a in range(2):
+        act(T.G[:, 512 * a:512 * a + 512], T.cp[:, :].indirect(T.lu[:, 32 * a:32 * a + 32]), F.Identity, 0.0, 1.0,
+            [al("cp"), al("lu")], [("G", 512 * a, 512 * a + 512)])
+    mm(to_list("psD", 0, "W0", "cel", 0, C, True, False), [al("W0"), al("cel")], [al("psD")])
+    mm([(T.psA[:, 0:256], T.I[:], T.cel[:, 512:768], True, False)], [al("I"), al("cel")], [al("psA")])
+    mm([(T.psB[:, 0:256], T.I[:], T.cel[:, 768:1024], True, False)], [al("I"), al("cel")], [al("psB")])
+    ts(T.wa[:], T.sf[:], 1.0, -1.0, A.is_equal, A.mult, [al("sf")], [al("wa")])
+    ts(T.wb[:], T.sf[:], 2.0, -256.0, A.is_equal, A.mult, [al("sf")], [al("wb")])
+    ts(T.BO[:], T.Xg[:], T.gs[:], None, A.is_equal, None, [al("Xg"), al("gs")], [al("BO")])
+    ts(T.ta[:], T.X[:, 0:128], T.kf[:], None, A.is_gt, None, [al("X"), al("kf")], [al("ta")])
+    ts(T.tc[:], T.X[:, 0:128], T.kf[:], float(BIG), A.is_equal, A.mult, [al("X"), al("kf")], [al("tc")])
+    tt(T.wk[:], T.wa[:], T.wb[:], A.add, [al("wa"), al("wb")], [al("wk")])
+    tt(T.td[:], T.ta[:], T.BO[:], A.mult, [al("ta"), al("BO")], [al("td")])
+    for a in range(2):
+        tt(T.Sel[:, 512 * a:512 * a + 512], T.I16[:, :].indirect(T.hu[:, 32 * a:32 * a + 32]), T.G[:, 512 * a:512 * a + 512],
+           A.mult, [al("I16"), al("hu"), ("G", 512 * a, 512 * a + 512)], [("Sel", 512 * a, 512 * a + 512)])
+    mm(to_list("psD", 0, "W1", "Sel", 0, C, False, True), [al("W1"), al("Sel")], [al("psD")])
+    tt(T.L[:], T.td[:], T.tc[:], A.add, [al("td"), al("tc")], [al("L")])
+    x0 = (-KB * rank) % 32
+    ts(T.P5[:, 0:480:5], T.Dio[:, x0:x0 + 96], T.gs[:], None, A.subtract, None, [al("Dio"), al("gs")], [("P5", 0, 1)])
+    tt(T.U[:], T.BO[:], T.L[:], A.subtract, [al("BO"), al("L")], [al("U")])
+
+    def places(k, sign, rot, between=None):
+        parts = [(0, rot, k - rot)] + ([(k - rot, 0, rot)] if rot else [])
+        for (x, c, m) in parts:
+            ts(T.li[:, c:c + m], T.psD[:, x:x + m], sign, 256.0, A.mult, A.add, [al("psD")], [("li", c, c + m)])
+        ts(T.la[:, 0:k], T.li[:, 0:k], 1027, None, A.bitwise_and, None, [al("li")], [al("la")])
+        for q in range(N):
+            e = ("E", 96 * q, 96 * q + 96)
+            ts(T.E[:, 96 * q:96 * q + k], T.la[:, 0:k], float(q), None, A.is_equal, None, [al("la")], [e])
+            ps = T["psP%d" % q]
+            mm([(ps[:, 0:k], T.L[:], T.E[:, 96 * q:96 * q + k], True, False),
+                (ps[:, 1:k], T.U[:], T.E[:, 96 * q:96 * q + k - 1], False, True)], [al("L"), al("U"), e], [al("psP%d" % q)])
+        if between is not None:
+            between()
+        for q in range(N):
+            op("v", lambda q=q: V.tensor_tensor_scan(T.P5[:, q + 1:5 * k:5], T["psP%d" % q][:, 0:k], T.m5[:, 4:5 * k:5],
+                                                    float(DUMP - BIG + CAP * q), A.add, A.min),
+               [al("psP%d" % q), al("m5")], [("P5", q + 1, q + 2)])
+        op("v", lambda: V.tensor_tensor_scan(T.M5[:, 0:5 * k], T.m5[:, 0:5 * k], T.P5[:, 0:5 * k], 0.0, A.min, A.max),
+           [al("m5"), al("P5")], [al("M5")])
+        for (x, c, m) in parts:
+            cpy(T.pu[:, x:x + m], T.M5[:, 5 * c + 4:5 * (c + m):5], [al("M5")], [("pu", x, x + m)])
+
+    def back(ps, lo, hi, sn, dst, sd, st):
+        k = hi - lo
+        act(T.sg[:, lo:hi], T[ps][:, 0:k], F.Sign, -0.5, sn, [al(ps)], [("sg", lo, hi)])
+        act(T[dst][:, lo:hi], T[ps][:, 0:k], F.Identity, 0.0, sd, [al(ps)], [(dst, lo, hi)])
+        act(T.t[:, lo:hi], T.sg[:, lo:hi], F.Identity, 128.0 * st, 128.0 * st, [("sg", lo, hi)], [("t", lo, hi)])
+
+    def scatter(h, src, lo, hi):
+        w = "win%d" % h
+        tt(T[w][:, :].indirect(T.pu[:, lo // 16:hi // 16]), T[src][:, lo:hi], T.t[:, lo:hi], A.add,
+           [(src, lo, hi), ("t", lo, hi), ("pu", lo // 16, hi // 16)], [al(w)])
+
+    peers = [q for q in range(N) if q != rank]
+
+    def send(h):
+        w = "win%d" % h
+        far = [q for q in peers if topo.die(T.cores[q]) != topo.die(core)]
+        near = [q for q in peers if q not in far]
+        trs = []
+        for q in peers:
+            eng = topo.engines(core, T.cores[q])
+            if q in far:
+                i = far.index(q)
+                use = eng[0::2][4 * i:4 * i + 4]
+            else:
+                i = near.index(q)
+                use = eng[1::2][4 * i:4 * i + 4]
+            m = 0
+            for e in use:
+                m |= 1 << e
+            rid, pid, _se = topo.addr(T.cores[q])
+            slot = (rank - q) % N if h < H - 1 else rank
+            trs.append(RemoteDMATransfer(dst_ids=[DstId(rid=rid, pnc=pid)], dma_engine_mask=m,
+                                         remote_sem=T.sem["ar%d" % h if h < H - 1 else "al%d" % rank],
+                                         src=T[w][:, DUMP + CAP * q:DUMP + CAP * (q + 1)],
+                                         dst=T["R%d" % h][:, CAP * slot:CAP * (slot + 1)]))
+        need("g", [k[5] for k in log if k[0] == w and k[3]][-1])
+        g.remote_dma_fused(trs, local_sem=T.sem["ls%d" % h])
+        count["ls%d" % h] = 4 * len(peers)
+        return ("ls%d" % h, 4 * len(peers), dict(known["g"]))
+
+    places(64, 1.0, 0, lambda: ts(T.Wk[:], T.X[:], T.c15[:], T.wk[:], A.is_equal, A.mult,
+                                  [al("X"), al("c15"), al("wk")], [al("Wk")]))
+    tt(T.n[:, 0:512], T.pad[:, :].indirect(T.ku[:, 0:32]), T.cel[:, 0:512], A.subtract,
+       [al("pad"), al("ku"), al("cel")], [("n", 0, 512)])
+    for lo, ps in ((512, "psA"), (768, "psB")):
+        act(T.d[:, lo:lo + 256], T.pad[:, :].indirect(T.ku[:, lo // 16:lo // 16 + 16]), F.Identity, 0.0, -1.0,
+            [al("pad"), al("ku")], [("d", lo, lo + 256)])
+        mm([(T[ps][:, 0:256], T.I[:], T.d[:, lo:lo + 256], False, True)], [al("I"), ("d", lo, lo + 256)], [al(ps)])
+    ts(T.t[:, 0:512], T.n[:, 0:512], 0.0, -256.0, A.is_gt, A.mult, [("n", 0, 512)], [("t", 0, 512)])
+    back("psA", 512, 768, -1.0, "n", -1.0, -1.0)
+    back("psB", 768, 1024, -1.0, "n", -1.0, -1.0)
+    scatter(0, "n", 0, 512)
+    scatter(0, "n", 512, 768)
+    scatter(0, "n", 768, 1024)
+    sent = send(0)
+    iota(T.win2[:, DUMP:], [[0, S]], 0, 0, [al("win2")])
+
+    A0, A1, V0 = CAP, 640, 960
+
+    def keys(src, lo, hi, c0):
+        k = (hi - lo) // 16
+        mm(to_list("psK", c0, "Wk", src, lo, hi, True, True), [al("Wk"), (src, lo, hi)], [al("psK")])
+        cpy(T.li[:, c0:c0 + k], T.psK[:, c0:c0 + k], [al("psK")], [("li", c0, c0 + k)])
+        ts(T.la[:, c0:c0 + k], T.li[:, c0:c0 + k], P - 1, None, A.bitwise_and, None, [("li", c0, c0 + k)], [("la", c0, c0 + k)])
+        cpy(T.ku[:, c0:c0 + k], T.la[:, c0:c0 + k], [("la", c0, c0 + k)], [("ku", c0, c0 + k)])
+
+    def by_vector(src, slo, lo, hi):
+        tt(T.n[:, lo:hi], T.pad[:, :].indirect(T.ku[:, lo // 16:hi // 16]), T[src][:, slo:slo + hi - lo], A.add,
+           [al("pad"), ("ku", lo // 16, hi // 16), (src, slo, slo + hi - lo)], [("n", lo, hi)])
+
+    def fold(lo, hi, last):
+        ts(T.t[:, lo:hi], T.n[:, lo:hi], 0.0, 256.0 if last else -256.0, A.is_gt, A.mult, [("n", lo, hi)], [("t", lo, hi)])
+        if last:
+            ts(T.d[:, lo:hi], T.n[:, lo:hi], -1.0, None, A.mult, None, [("n", lo, hi)], [("d", lo, hi)])
+
+    for h in range(1, H):
+        last = h == H - 1
+        st = 1.0 if last else -1.0
+        src = "d" if last else "n"
+        Rn, wp = "R%d" % (h - 1), "win%d" % (h - 1)
+        R = T[Rn]
+        o = DUMP + CAP * rank
+        keys(wp, o, o + CAP, 0)
+        by_vector(wp, o, 0, CAP)
+        act(R[:, 0:CAP], T.n[:, 0:CAP], F.Identity, 0.0, 1.0, [("n", 0, CAP)], [(Rn, 0, CAP)])
+        fold(0, CAP, last)
+        count["ar%d" % (h - 1)] = 4 * len(peers)
+        log.append((Rn, CAP, S, True, "dma", ("ar%d" % (h - 1), 4 * len(peers), {})))
+        keys(Rn, CAP, S, KB)
+        mm([(T.psD[:, 0:96], T.Z[:], R[:, CAP:CAP + 96], True, False)] + to_list("psD", 0, "W0", Rn, 0, V0, False, False),
+           [al("Z"), al("W0"), al(Rn)], [al("psD")])
+        mm([(T.psA[:, 0:A1 - A0], T.I[:], R[:, A0:A1], True, False)], [al("I"), (Rn, A0, A1)], [al("psA")])
+        act(T.n[:, A0:V0], T.pad[:, :].indirect(T.ku[:, A0 // 16:V0 // 16]), F.Identity, 0.0, 1.0,
+            [al("pad"), ("ku", A0 // 16, V0 // 16)], [("n", A0, V0)])
+        by_vector(Rn, V0, V0, S)
+        mm(to_list("psD", KB, "W0", "n", CAP, S, False, True), [al("W0"), ("n", CAP, S)], [al("psD")])
+        mm([(T.psA[:, 0:A1 - A0], T.I[:], T.n[:, A0:A1], False, True)], [al("I"), ("n", A0, A1)], [al("psA")])
+        fold(V0, S, last)
+        back("psA", A0, A1, 1.0, src, -st, st)
+
+        def second(R=R, Rn=Rn, src=src, st=st):
+            mm([(T.psB[:, 0:V0 - A1], T.I[:], R[:, A1:V0], True, False),
+                (T.psB[:, 0:V0 - A1], T.I[:], T.n[:, A1:V0], False, True)],
+               [al("I"), (Rn, A1, V0), ("n", A1, V0)], [al("psB")])
+            back("psB", A1, V0, 1.0, src, -st, st)
+        places(96, -1.0, KB * rank, second)
+        for lo in (2 * DUMP, 0, DUMP):
+            scatter(h, src, lo, lo + DUMP)
+        sent = send(h)
+
+    wl, Rl = "win%d" % (H - 1), T["R%d" % (H - 1)]
+
+    def store(qn, q, after=()):
+        lo, hi = CAP * q, CAP * (q + 1)
+        tok = op(qn, lambda: Q[qn].dma_start(T.y[:, lo:hi], T.yf[:, lo:hi]), [("yf", lo, hi)], (), sem="st%d" % q, inc=16, after=after)
+        return qn, tok
+
+    lo = CAP * rank
+    act(T.yf[:, lo:lo + CAP], T[wl][:, DUMP + lo:DUMP + lo + CAP], F.Identity, 0.0, 1.0, [al(wl)], [("yf", lo, lo + CAP)])
+    stores = [store("s", rank, [sent])]
+    for q in peers:
+        count["al%d" % q] = 4
+        log.append(("Rl", CAP * q, CAP * (q + 1), True, "dma", ("al%d" % q, 4, {})))
+    order = sorted(peers, key=lambda q: topo.die(T.cores[q]) != topo.die(core))
+
+    def widen(qn, lo, hi):
+        if qn == "v":
+            cpy(T.yf[:, lo:hi], Rl[:, lo:hi], [("Rl", lo, hi)], [("yf", lo, hi)])
+        else:
+            act(T.yf[:, lo:hi], Rl[:, lo:hi], F.Identity, 0.0, 1.0, [("Rl", lo, hi)], [("yf", lo, hi)])
+    for q in order:
+        widen("v", CAP * q, CAP * q + CAP // 2)
+        widen("a", CAP * q + CAP // 2, CAP * (q + 1))
+        if q != order[-1]:
+            stores.append(store("s", q))
+    stores.append(store("a", order[-1]))
+    for qn, tok in stores:
+        need(qn, tok)
+    for s_, v_ in count.items():
+        if waited.get(s_, 0) < v_:
+            g.wait_ge(T.sem[s_], v_)

@@ -7,38 +7,48 @@ DUMP = 512
 BIG = 2048
 EMPTY = -1024
 KB = CAP // 16
+LIFT = 288.0
+XV = 320
+OV, A1, V0, V1 = 224, 576, 960, 1248
 
 bf, f16, f32, i32, u16 = "bfloat16", "float16", "float32", "int32", "uint16"
 SCRATCH = {
-    "pad": ("sbuf", [128, P], bf), "cel": ("sbuf", [128, C], bf), "fi": ("sbuf", [128, 64], i32),
-    "cp": ("sbuf", [128, 512], bf),
-    "X": ("sbuf", [128, 144], f32), "Xg": ("sbuf", [128, 128], f32), "Dio": ("sbuf", [128, 128], f32),
-    "pk": ("sbuf", [128, 1], i32), "gsi": ("sbuf", [128, 1], i32),
-    "kf": ("sbuf", [128, 1], f32), "gs": ("sbuf", [128, 1], f32), "sf": ("sbuf", [128, 1], f32),
+    "pad": ("sbuf", [128, P + 16], bf), "cel": ("sbuf", [128, C], bf), "fi": ("sbuf", [128, 64], i32),
+    "cp": ("sbuf", [128, 512], bf), "c0": ("sbuf", [8, C], bf), "c1": ("sbuf", [128, XV], bf),
+    "one": ("sbuf", [128, 144], bf), "X": ("sbuf", [128, 144], f32), "Dio": ("sbuf", [128, 128], f32),
+    "pk": ("sbuf", [128, 1], i32), "si": ("sbuf", [128, 1], i32),
+    "kf": ("sbuf", [128, 1], f32), "sf": ("sbuf", [128, 1], f32),
     "c15": ("sbuf", [128, 1], f32), "w0": ("sbuf", [128, 1], f32), "wa": ("sbuf", [128, 1], f32),
     "wb": ("sbuf", [128, 1], f32), "wk": ("sbuf", [128, 1], f32),
-    "W0": ("sbuf", [128, 144], bf), "W1": ("sbuf", [128, 144], bf), "Wk": ("sbuf", [128, 144], bf),
-    "I": ("sbuf", [128, 128], bf), "I16": ("sbuf", [128, 16], bf), "Z": ("sbuf", [128, 128], bf),
-    "BO": ("sbuf", [128, 128], f16), "ta": ("sbuf", [128, 128], f16), "tc": ("sbuf", [128, 128], f16),
-    "td": ("sbuf", [128, 128], f16), "L": ("sbuf", [128, 128], f16), "U": ("sbuf", [128, 128], f16),
+    "W0": ("sbuf", [128, 144], bf), "W1": ("sbuf", [128, 144], bf), "Wk": ("sbuf", [128, 144], bf), "W8": ("sbuf", [8, 144], bf),
+    "I": ("sbuf", [128, 128], bf), "J": ("sbuf", [128, 128], bf), "NI": ("sbuf", [128, 128], bf),
+    "I16": ("sbuf", [128, 16], bf), "Z": ("sbuf", [128, 128], bf), "CL": ("sbuf", [128, CAP], bf),
+    "ta": ("sbuf", [128, 128], bf), "tc": ("sbuf", [128, 128], bf), "td": ("sbuf", [128, 128], bf), "te": ("sbuf", [128, 128], bf),
+    "L": ("sbuf", [128, 128], f16), "U": ("sbuf", [128, 128], f16),
     "m5": ("sbuf", [128, 480], bf), "P5": ("sbuf", [128, 480], f16), "M5": ("sbuf", [128, 480], f16),
     "E": ("sbuf", [128, 384], f16),
     "li": ("sbuf", [128, 96], i32), "la": ("sbuf", [128, 96], i32), "lb": ("sbuf", [128, 96], i32),
-    "ku": ("sbuf", [128, 96], u16), "lu": ("sbuf", [128, 64], u16), "hu": ("sbuf", [128, 64], u16),
+    "ku": ("sbuf", [128, 64], u16), "lu": ("sbuf", [128, 64], u16), "hu": ("sbuf", [128, 64], u16),
     "pu": ("sbuf", [128, 96], u16),
     "G": ("sbuf", [128, C], bf), "Sel": ("sbuf", [128, C], bf),
     "n": ("sbuf", [128, S], bf), "t": ("sbuf", [128, S], bf), "d": ("sbuf", [128, S], bf), "sg": ("sbuf", [128, S], bf),
-    "yf": ("sbuf", [128, S], f32),
+    "xs": ("sbuf", [128, S], f32), "yf": ("sbuf", [128, S], f32),
     "psK": ("psum", [128, 512], f32), "psD": ("psum", [128, 512], f32),
     "psA": ("psum", [128, 512], f32), "psB": ("psum", [128, 512], f32),
 }
 for _h in range(H):
     SCRATCH["win%d" % _h] = ("sbuf", [128, DUMP + S], bf)
     SCRATCH["R%d" % _h] = ("sbuf", [128, S], bf)
+for _h in range(H - 1):
+    SCRATCH["ko%d" % _h] = ("sbuf", [128, (N - 1) * KB], u16)
+    SCRATCH["kn%d" % _h] = ("sbuf", [128, N * KB], u16)
+    SCRATCH["ws%d" % (_h + 1)] = ("sbuf", [128, DUMP + S], f32)
+    SCRATCH["wc%d" % (_h + 1)] = ("sbuf", [128, S], bf)
 for _q in range(N):
     SCRATCH["psP%d" % _q] = ("psum", [128, 512], f32)
 
-SEMAPHORES = (["cv", "ca", "cp", "cg", "dfi", "dcp", "dcel", "dpad", "ar0", "ar1", "ls0", "ls1", "ls2"]
+SEMAPHORES = (["cv", "ca", "cp", "cg", "dfi", "dcp", "dc0", "dcel", "dcem", "dpad", "ar0", "ar1", "ak0", "ak1",
+               "ls0", "ls1", "ls2", "lk0", "lk1"]
               + ["al%d" % q for q in range(N)] + ["st%d" % q for q in range(N)])
 
 
@@ -62,9 +72,9 @@ def rank_program(g, core, T, topo):
             if known[q].get(s_, 0) < v_:
                 known[q][s_] = v_
 
-    def op(q, fn, r=(), w=(), sem=None, inc=1, after=()):
+    def op(q, fn, r=(), w=(), sem=None, inc=1):
         eng = q if sem is None else "dma"
-        toks = list(after)
+        toks = []
         for acc, wr in [(x, False) for x in r] + [(x, True) for x in w]:
             for (b, lo, hi, owr, oq, tok) in log:
                 if b != acc[0] or hi <= acc[1] or acc[2] <= lo:
@@ -105,7 +115,12 @@ def rank_program(g, core, T, topo):
     def cpy(out, in_, r, w):
         return op("v", lambda: V.tensor_copy(out, in_), r, w)
 
+    def fill(out, value, w):
+        return op("v", lambda: V.memset(out, value), (), w)
+
     def act(out, in_, func, bias, scale, r, w):
+        if bias is None:
+            return op("a", lambda: ACT.activation(out, in_, func), r, w)
         return op("a", lambda: ACT.activation(out, in_, func, bias=bias, scale=scale), r, w)
 
     def iota(out, pattern, base, cm, w, flag=True):
@@ -113,13 +128,21 @@ def rank_program(g, core, T, topo):
             return op("g", lambda: g.iota(out, pattern, base, cm, allow_small_or_imprecise_dtypes=True), (), w)
         return op("g", lambda: g.iota(out, pattern, base, cm), (), w)
 
-    def mm(calls, r, w, after=()):
+    def select(out, in_, pattern, cmp, other, base, cm, r, w):
+        return op("g", lambda: g.affine_select(out, in_, pattern, cmp, other, base, cm), r, w)
+
+    def mm(calls, r, w):
         def run():
             ins = None
             for (o, l, x, st, sp) in calls:
                 ins = PE.matmul(o, l, x, st, sp)
             return ins
-        return op("p", run, r, w, after=after)
+        return op("p", run, r, w)
+
+    def add_up(ps, terms, start=True, stop=True):
+        mm([(T[ps][:, 0:hi - lo], T[wt][:], T[b][:, lo:hi], start and i == 0, stop and i == len(terms) - 1)
+            for i, (wt, b, lo, hi) in enumerate(terms)],
+           [al(wt) for (wt, b, lo, hi) in terms] + [(b, lo, hi) for (wt, b, lo, hi) in terms], [al(ps)])
 
     def to_list(ps, c0, W, src, lo, hi, start, stop):
         k = (hi - lo) // 16
@@ -127,61 +150,65 @@ def rank_program(g, core, T, topo):
                 for r in range(16)]
 
     op("s", lambda: g.sync.dma_start(T.fi[:], T.first[:]), (), [al("fi")], sem="dfi", inc=16)
-    op("a", lambda: g.scalar.dma_start(T.cel[:], T.cells[:]), (), [al("cel")], sem="dcel", inc=16)
-    op("s", lambda: g.sync.dma_start(T.cp[:], T.pads[0:128:16, :]), (), [al("cp")], sem="dcp", inc=16)
-    op("s", lambda: g.sync.dma_start(T.pad[:], T.pads[:]), (), [al("pad")], sem="dpad", inc=16)
+    op("a", lambda: g.scalar.dma_start(T.cp[:], T.pads[0:128:16, :]), (), [al("cp")], sem="dcp", inc=16)
+    op("a", lambda: g.scalar.dma_start(T.c0[:], T.cells[0:128:16, :]), (), [al("c0")], sem="dc0", inc=16)
+    op("s", lambda: g.sync.dma_start(T.cel[:, 0:XV], T.cells[:, 0:XV]), (), [("cel", 0, XV)], sem="dcel", inc=16)
+    op("s", lambda: g.sync.dma_start(T.pad[:, 0:P], T.pads[:]), (), [("pad", 0, P)], sem="dpad", inc=16)
+    op("s", lambda: g.sync.dma_start(T.cel[:, XV:C], T.cells[:, XV:C]), (), [("cel", XV, C)], sem="dcem", inc=16)
 
+    col, grp = [[1, 128]], [[16, 8], [0, 16]]
+    ncol, ngrp = [[-1, 128]], [[-16, 8], [0, 16]]
+    fill(T.one[:], 1.0, [al("one")])
     iota(T.pk[:], [[0, 1]], 0, 1, [al("pk")], False)
-    iota(T.kf[:], [[0, 1]], 0, 1, [al("kf")])
     iota(T.X[:], [[1, 144]], 0, 0, [al("X")])
-    iota(T.Xg[:], [[16, 8], [0, 16]], 0, 0, [al("Xg")])
-    iota(T.Dio[:], [[0, 4], [16, 32]], 0, 1, [al("Dio")])
+    iota(T.kf[:], [[0, 1]], 15, 1, [al("kf")])
+    select(T.W8[:], T.one[0:8, :], [[1, 144]], A.is_equal, 0.0, -15, -16, [al("one")], [al("W8")])
+    select(T.ta[:], T.one[:, 0:128], ngrp, A.is_ge, 0.0, 0, 1, [al("one")], [al("ta")])
+    select(T.tc[:], T.one[:, 0:128], grp, A.is_ge, 0.0, 15, -1, [al("one")], [al("tc")])
+    select(T.td[:], T.ta[:], col, A.is_gt, 0.0, 0, -1, [al("ta")], [al("td")])
+    select(T.te[:], T.tc[:], ncol, A.is_gt, 0.0, 0, 1, [al("tc")], [al("te")])
+    iota(T.Dio[:], [[0, 4], [16, 32]], 0, 0, [al("Dio")])
+    select(T.I[:], T.one[:, 0:128], col, A.is_equal, 0.0, 0, -1, [al("one")], [al("I")])
+    select(T.L[:], T.td[:], col, A.not_equal, float(BIG), 0, -1, [al("td")], [al("L")])
+    select(T.U[:], T.te[:], col, A.not_equal, float(1 - BIG), 0, -1, [al("te")], [al("U")])
     iota(T.m5[:], [[0, 96], [4096, 5]], 0, 0, [al("m5")])
-    iota(T.win0[:, DUMP:], [[0, S]], EMPTY, 0, [al("win0")])
-    iota(T.win1[:, DUMP:], [[0, S]], EMPTY, 0, [al("win1")])
+    iota(T.win1[:, DUMP:], [[0, S]], 0, 0, [al("win1")])
 
-    op("v", lambda: V.memset(T.Z[:], 0.0), (), [al("Z")])
-    ts(T.gsi[:], T.pk[:], 112, None, A.bitwise_and, None, [al("pk")], [al("gsi")])
-    cpy(T.gs[:], T.gsi[:], [al("gsi")], [al("gs")])
-    ts(T.sf[:], T.kf[:], T.gs[:], None, A.subtract, None, [al("kf"), al("gs")], [al("sf")])
-    ts(T.c15[:], T.gs[:], 15.0, None, A.add, None, [al("gs")], [al("c15")])
-    ts(T.w0[:], T.sf[:], 0.0, None, A.is_equal, None, [al("sf")], [al("w0")])
+    ts(T.si[:], T.pk[:], 15, None, A.bitwise_and, None, [al("pk")], [al("si")])
+    cpy(T.sf[:], T.si[:], [al("si")], [al("sf")])
+    fill(T.win0[:, DUMP:], 0.0, [al("win0")])
     ts(T.I16[:], T.X[:, 0:16], T.sf[:], None, A.is_equal, None, [al("X"), al("sf")], [al("I16")])
-    ts(T.W1[:], T.X[:], T.c15[:], -1.0, A.is_equal, A.mult, [al("X"), al("c15")], [al("W1")])
-    ts(T.W0[:], T.X[:], T.c15[:], T.w0[:], A.is_equal, A.mult, [al("X"), al("c15"), al("w0")], [al("W0")])
-    ts(T.I[:], T.X[:, 0:128], T.kf[:], None, A.is_equal, None, [al("X"), al("kf")], [al("I")])
 
     ts(T.la[:, 0:64], T.fi[:], 511, None, A.bitwise_and, None, [al("fi")], [al("la")])
     ts(T.lb[:, 0:64], T.fi[:], 9, None, A.logical_shift_right, None, [al("fi")], [al("lb")])
     cpy(T.lu[:], T.la[:, 0:64], [al("la")], [al("lu")])
     cpy(T.hu[:], T.lb[:, 0:64], [al("lb")], [al("hu")])
-    cpy(T.ku[:, 0:64], T.fi[:], [al("fi")], [al("ku")])
-    for a in range(2):
-        act(T.G[:, 512 * a:512 * a + 512], T.cp[:, :].indirect(T.lu[:, 32 * a:32 * a + 32]), F.Identity, 0.0, 1.0,
-            [al("cp"), al("lu")], [("G", 512 * a, 512 * a + 512)])
-    mm(to_list("psD", 0, "W0", "cel", 0, C, True, False), [al("W0"), al("cel")], [al("psD")])
-    mm([(T.psA[:, 0:256], T.I[:], T.cel[:, 512:768], True, False)], [al("I"), al("cel")], [al("psA")])
-    mm([(T.psB[:, 0:256], T.I[:], T.cel[:, 768:1024], True, False)], [al("I"), al("cel")], [al("psB")])
-    ts(T.wa[:], T.sf[:], 1.0, -1.0, A.is_equal, A.mult, [al("sf")], [al("wa")])
-    ts(T.wb[:], T.sf[:], 2.0, -256.0, A.is_equal, A.mult, [al("sf")], [al("wb")])
-    ts(T.BO[:], T.Xg[:], T.gs[:], None, A.is_equal, None, [al("Xg"), al("gs")], [al("BO")])
-    ts(T.ta[:], T.X[:, 0:128], T.kf[:], None, A.is_gt, None, [al("X"), al("kf")], [al("ta")])
-    ts(T.tc[:], T.X[:, 0:128], T.kf[:], float(BIG), A.is_equal, A.mult, [al("X"), al("kf")], [al("tc")])
-    tt(T.wk[:], T.wa[:], T.wb[:], A.add, [al("wa"), al("wb")], [al("wk")])
-    tt(T.td[:], T.ta[:], T.BO[:], A.mult, [al("ta"), al("BO")], [al("td")])
-    for a in range(2):
-        tt(T.Sel[:, 512 * a:512 * a + 512], T.I16[:, :].indirect(T.hu[:, 32 * a:32 * a + 32]), T.G[:, 512 * a:512 * a + 512],
-           A.mult, [al("I16"), al("hu"), ("G", 512 * a, 512 * a + 512)], [("Sel", 512 * a, 512 * a + 512)])
+    ts(T.c15[:], T.kf[:], T.sf[:], None, A.subtract, None, [al("kf"), al("sf")], [al("c15")])
+    cpy(T.ku[:], T.fi[:], [al("fi")], [al("ku")])
+    ts(T.W1[:], T.X[:], T.c15[:], -1.0, A.is_equal, A.mult, [al("X"), al("c15")], [al("W1")])
+    fill(T.pad[:, P:P + 16], float(EMPTY), [("pad", P, P + 16)])
+    for a in range(4):
+        act(T.G[:, 256 * a:256 * a + 256], T.cp[:, :].indirect(T.lu[:, 16 * a:16 * a + 16]), F.Identity, 0.0, 1.0,
+            [al("cp"), al("lu")], [("G", 256 * a, 256 * a + 256)])
+    act(T.c1[:], T.cel[:, 0:XV], F.Identity, 1.0, 1.0, [("cel", 0, XV)], [al("c1")])
+    mm([(T.psD[:, 0:64], T.W8[:, 15 - r:143 - r], T.c0[:, r:C:16], r == 0, False) for r in range(16)],
+       [al("W8"), al("c0")], [al("psD")])
+    for a in range(4):
+        tt(T.Sel[:, 256 * a:256 * a + 256], T.I16[:, :].indirect(T.hu[:, 16 * a:16 * a + 16]), T.G[:, 256 * a:256 * a + 256],
+           A.mult, [al("I16"), al("hu"), ("G", 256 * a, 256 * a + 256)], [("Sel", 256 * a, 256 * a + 256)])
     mm(to_list("psD", 0, "W1", "Sel", 0, C, False, True), [al("W1"), al("Sel")], [al("psD")])
-    tt(T.L[:], T.td[:], T.tc[:], A.add, [al("td"), al("tc")], [al("L")])
     x0 = (-KB * rank) % 32
-    ts(T.P5[:, 0:480:5], T.Dio[:, x0:x0 + 96], T.gs[:], None, A.subtract, None, [al("Dio"), al("gs")], [("P5", 0, 1)])
-    tt(T.U[:], T.BO[:], T.L[:], A.subtract, [al("BO"), al("L")], [al("U")])
+    ts(T.P5[:, 0:480:5], T.Dio[:, x0:x0 + 96], T.sf[:], None, A.add, None, [al("Dio"), al("sf")], [("P5", 0, 1)])
+    ts(T.wa[:], T.sf[:], 1.0, None, A.is_equal, None, [al("sf")], [al("wa")])
+    ts(T.wb[:], T.sf[:], 2.0, 256.0, A.is_equal, A.mult, [al("sf")], [al("wb")])
+    tt(T.wk[:], T.wa[:], T.wb[:], A.add, [al("wa"), al("wb")], [al("wk")])
+    tt(T.n[:, 0:XV], T.pad[:, :].indirect(T.ku[:, 0:XV // 16]), T.c1[:], A.subtract,
+       [al("pad"), al("ku"), al("c1")], [("n", 0, XV)])
 
-    def places(k, sign, rot, between=None):
+    def places(k, sign, base, rot, between):
         parts = [(0, rot, k - rot)] + ([(k - rot, 0, rot)] if rot else [])
         for (x, c, m) in parts:
-            ts(T.li[:, c:c + m], T.psD[:, x:x + m], sign, 256.0, A.mult, A.add, [al("psD")], [("li", c, c + m)])
+            ts(T.li[:, c:c + m], T.psD[:, x:x + m], sign, base, A.mult, A.add, [al("psD")], [("li", c, c + m)])
         ts(T.la[:, 0:k], T.li[:, 0:k], 1027, None, A.bitwise_and, None, [al("li")], [al("la")])
         for q in range(N):
             e = ("E", 96 * q, 96 * q + 96)
@@ -189,22 +216,18 @@ def rank_program(g, core, T, topo):
             ps = T["psP%d" % q]
             mm([(ps[:, 0:k], T.L[:], T.E[:, 96 * q:96 * q + k], True, False),
                 (ps[:, 1:k], T.U[:], T.E[:, 96 * q:96 * q + k - 1], False, True)], [al("L"), al("U"), e], [al("psP%d" % q)])
-        if between is not None:
-            between()
+        between()
         for q in range(N):
             op("v", lambda q=q: V.tensor_tensor_scan(T.P5[:, q + 1:5 * k:5], T["psP%d" % q][:, 0:k], T.m5[:, 4:5 * k:5],
-                                                    float(DUMP - BIG + CAP * q), A.add, A.min),
+                                                    float(DUMP - BIG + CAP * ((q - rank) % N)), A.add, A.min),
                [al("psP%d" % q), al("m5")], [("P5", q + 1, q + 2)])
         op("v", lambda: V.tensor_tensor_scan(T.M5[:, 0:5 * k], T.m5[:, 0:5 * k], T.P5[:, 0:5 * k], 0.0, A.min, A.max),
            [al("m5"), al("P5")], [al("M5")])
         for (x, c, m) in parts:
             cpy(T.pu[:, x:x + m], T.M5[:, 5 * c + 4:5 * (c + m):5], [al("M5")], [("pu", x, x + m)])
 
-    def back(ps, lo, hi, sn, dst, sd, st):
-        k = hi - lo
-        act(T.sg[:, lo:hi], T[ps][:, 0:k], F.Sign, -0.5, sn, [al(ps)], [("sg", lo, hi)])
-        act(T[dst][:, lo:hi], T[ps][:, 0:k], F.Identity, 0.0, sd, [al(ps)], [(dst, lo, hi)])
-        act(T.t[:, lo:hi], T.sg[:, lo:hi], F.Identity, 128.0 * st, 128.0 * st, [("sg", lo, hi)], [("t", lo, hi)])
+    def fold(src, lo, hi, last):
+        ts(T.t[:, lo:hi], T[src][:, lo:hi], 0.0, 256.0 if last else -256.0, A.is_ge, A.mult, [(src, lo, hi)], [("t", lo, hi)])
 
     def scatter(h, src, lo, hi):
         w = "win%d" % h
@@ -212,124 +235,174 @@ def rank_program(g, core, T, topo):
            [(src, lo, hi), ("t", lo, hi), ("pu", lo // 16, hi // 16)], [al(w)])
 
     peers = [q for q in range(N) if q != rank]
+    far = [q for q in peers if topo.die(T.cores[q]) != topo.die(core)]
+    near = [q for q in peers if q not in far]
 
-    def send(h):
-        w = "win%d" % h
-        far = [q for q in peers if topo.die(T.cores[q]) != topo.die(core)]
-        near = [q for q in peers if q not in far]
+    def lanes(q, wide):
+        eng = topo.engines(core, T.cores[q])
+        if q in far:
+            return eng[0::2][4 * far.index(q):4 * far.index(q) + 4]
+        return eng[1::2][0:8 if wide else 4]
+
+    def fused(to, src, dst, width, rsem, lsem, slot, wide):
         trs = []
-        for q in peers:
-            eng = topo.engines(core, T.cores[q])
-            if q in far:
-                i = far.index(q)
-                use = eng[0::2][4 * i:4 * i + 4]
-            else:
-                i = near.index(q)
-                use = eng[1::2][4 * i:4 * i + 4]
-            m = 0
-            for e in use:
-                m |= 1 << e
+        for q in to:
             rid, pid, _se = topo.addr(T.cores[q])
-            slot = (rank - q) % N if h < H - 1 else rank
-            trs.append(RemoteDMATransfer(dst_ids=[DstId(rid=rid, pnc=pid)], dma_engine_mask=m,
-                                         remote_sem=T.sem["ar%d" % h if h < H - 1 else "al%d" % rank],
-                                         src=T[w][:, DUMP + CAP * q:DUMP + CAP * (q + 1)],
-                                         dst=T["R%d" % h][:, CAP * slot:CAP * (slot + 1)]))
+            trs.append(RemoteDMATransfer(dst_ids=[DstId(rid=rid, pnc=pid)], dma_engine_mask=sum(1 << e for e in lanes(q, wide)),
+                                         remote_sem=T.sem[rsem], src=src((q - rank) % N),
+                                         dst=T[dst][:, width * slot(q):width * (slot(q) + 1)]))
+        g.remote_dma_fused(trs, local_sem=T.sem[lsem])
+        count[lsem] = count.get(lsem, 0) + sum(len(lanes(q, wide)) for q in to)
+        return count[lsem]
+
+    def send(h, w, off, to):
+        last = h == H - 1
         need("g", [k[5] for k in log if k[0] == w and k[3]][-1])
-        g.remote_dma_fused(trs, local_sem=T.sem["ls%d" % h])
-        count["ls%d" % h] = 4 * len(peers)
-        return ("ls%d" % h, 4 * len(peers), dict(known["g"]))
+        tot = fused(to, lambda j: T[w][:, off + CAP * j:off + CAP * (j + 1)], "R%d" % h, CAP,
+                    "al%d" % rank if last else "ar%d" % h, "ls%d" % h,
+                    (lambda q: rank) if last else (lambda q: (rank - q) % N), h > 0)
+        if not last:
+            count["ar%d" % h] = tot
+            log.append(("R%d" % h, CAP, S, True, "dma", ("ar%d" % h, tot, {})))
 
-    places(64, 1.0, 0, lambda: ts(T.Wk[:], T.X[:], T.c15[:], T.wk[:], A.is_equal, A.mult,
-                                  [al("X"), al("c15"), al("wk")], [al("Wk")]))
-    tt(T.n[:, 0:512], T.pad[:, :].indirect(T.ku[:, 0:32]), T.cel[:, 0:512], A.subtract,
-       [al("pad"), al("ku"), al("cel")], [("n", 0, 512)])
-    for lo, ps in ((512, "psA"), (768, "psB")):
-        act(T.d[:, lo:lo + 256], T.pad[:, :].indirect(T.ku[:, lo // 16:lo // 16 + 16]), F.Identity, 0.0, -1.0,
-            [al("pad"), al("ku")], [("d", lo, lo + 256)])
-        mm([(T[ps][:, 0:256], T.I[:], T.d[:, lo:lo + 256], False, True)], [al("I"), ("d", lo, lo + 256)], [al(ps)])
-    ts(T.t[:, 0:512], T.n[:, 0:512], 0.0, -256.0, A.is_gt, A.mult, [("n", 0, 512)], [("t", 0, 512)])
-    back("psA", 512, 768, -1.0, "n", -1.0, -1.0)
-    back("psB", 768, 1024, -1.0, "n", -1.0, -1.0)
-    scatter(0, "n", 0, 512)
-    scatter(0, "n", 512, 768)
-    scatter(0, "n", 768, 1024)
-    sent = send(0)
-    iota(T.win2[:, DUMP:], [[0, S]], 0, 0, [al("win2")])
+    def keys(ps, src, lo, width, c0, dst):
+        k = width // 16
+        mm(to_list(ps, 0, "Wk", src, lo, lo + width, True, True), [al("Wk"), (src, lo, lo + width)], [al(ps)])
+        ts(T.li[:, c0:c0 + k], T[ps][:, 0:k], -257.0, None, A.add, None, [al(ps)], [("li", c0, c0 + k)])
+        ts(T.la[:, c0:c0 + k], T.li[:, c0:c0 + k], (P - 1) | (1 << 17), None, A.bitwise_and, None,
+           [("li", c0, c0 + k)], [("la", c0, c0 + k)])
+        return ts(T[dst][:, 0:k], T.la[:, c0:c0 + k], float(P), None, A.min, None, [("la", c0, c0 + k)], [(dst, 0, k)])
 
-    A0, A1, V0 = CAP, 640, 960
+    def send_keys(h, src, lo):
+        ko, kn = "ko%d" % h, "kn%d" % h
+        need("g", keys("psK", src, lo, S - CAP, KB, ko))
+        tot = fused(peers, lambda j: T[ko][:, KB * (j - 1):KB * j], kn, KB, "ak%d" % h, "lk%d" % h, lambda q: (rank - q) % N, h > 0)
+        count["ak%d" % h] = tot
+        log.append((kn, KB, N * KB, True, "dma", ("ak%d" % h, tot, {})))
 
-    def keys(src, lo, hi, c0):
-        k = (hi - lo) // 16
-        mm(to_list("psK", c0, "Wk", src, lo, hi, True, True), [al("Wk"), (src, lo, hi)], [al("psK")])
-        cpy(T.li[:, c0:c0 + k], T.psK[:, c0:c0 + k], [al("psK")], [("li", c0, c0 + k)])
-        ts(T.la[:, c0:c0 + k], T.li[:, c0:c0 + k], P - 1, None, A.bitwise_and, None, [("li", c0, c0 + k)], [("la", c0, c0 + k)])
-        cpy(T.ku[:, c0:c0 + k], T.la[:, c0:c0 + k], [("la", c0, c0 + k)], [("ku", c0, c0 + k)])
+    cuts = [(XV, XV + 256, "psA"), (XV + 256, XV + 512, "psB"), (XV + 512, C, "psK")]
 
-    def by_vector(src, slo, lo, hi):
-        tt(T.n[:, lo:hi], T.pad[:, :].indirect(T.ku[:, lo // 16:hi // 16]), T[src][:, slo:slo + hi - lo], A.add,
-           [al("pad"), ("ku", lo // 16, hi // 16), (src, slo, slo + hi - lo)], [("n", lo, hi)])
+    def pads_by_scalar(lo, hi, ps):
+        act(T.d[:, lo:hi], T.pad[:, :].indirect(T.ku[:, lo // 16:hi // 16]), F.Identity, 1.0, -1.0,
+            [al("pad"), al("ku")], [("d", lo, hi)])
 
-    def fold(lo, hi, last):
-        ts(T.t[:, lo:hi], T.n[:, lo:hi], 0.0, 256.0 if last else -256.0, A.is_gt, A.mult, [("n", lo, hi)], [("t", lo, hi)])
-        if last:
-            ts(T.d[:, lo:hi], T.n[:, lo:hi], -1.0, None, A.mult, None, [("n", lo, hi)], [("d", lo, hi)])
+    def back(lo, hi, ps):
+        act(T.sg[:, lo:hi], T[ps][:, 0:hi - lo], F.Sign, 0.5, -1.0, [al(ps)], [("sg", lo, hi)])
+        act(T.n[:, lo:hi], T[ps][:, 0:hi - lo], F.Identity, 0.0, -1.0, [al(ps)], [("n", lo, hi)])
+        act(T.t[:, lo:hi], T.sg[:, lo:hi], F.Identity, -128.0, -128.0, [("sg", lo, hi)], [("t", lo, hi)])
 
+    def add_cells(lo, hi, ps):
+        add_up(ps, [("I", "cel", lo, hi), ("I", "d", lo, hi)])
+    pads_by_scalar(*cuts[0])
+    pads_by_scalar(*cuts[1])
+    add_cells(*cuts[0])
+    back(*cuts[0])
+    pads_by_scalar(*cuts[2])
+    places(64, 1.0, 256.0, 0, lambda: fold("n", 0, XV, False))
+    add_cells(*cuts[1])
+    add_cells(*cuts[2])
+    back(*cuts[1])
+    back(*cuts[2])
+    for lo, hi in ((0, DUMP), (DUMP, C)):
+        scatter(0, "n", lo, hi)
+    act(T.Wk[:], T.W1[:], F.Identity, 0.0, T.wk[:], [al("W1"), al("wk")], [al("Wk")])
+    ts(T.w0[:], T.sf[:], 0.0, -1.0, A.is_equal, A.mult, [al("sf")], [al("w0")])
+    fill(T.Z[:], 0.0, [al("Z")])
+    act(T.W0[:], T.W1[:], F.Identity, 0.0, T.w0[:], [al("W1"), al("w0")], [al("W0")])
+    act(T.J[:], T.I[:], F.Identity, 0.0, -128.0, [al("I")], [al("J")])
+    act(T.NI[:], T.I[:], F.Identity, 0.0, -1.0, [al("I")], [al("NI")])
+    act(T.CL[:], T.pad[:, 0:CAP], F.Identity, -LIFT, 0.0, [al("pad")], [al("CL")])
+    act(T.ws1[:, DUMP:], T.pad[:, 0:S], F.Silu, LIFT, 0.0, [al("pad")], [al("ws1")])
+    send(0, "win0", DUMP, peers)
+    send_keys(0, "win0", DUMP + CAP)
+    iota(T.ws2[:, DUMP:], [[0, S]], int(LIFT), 0, [al("ws2")])
+
+    def by_vector(kn, src, slo, dst, lo, hi):
+        tt(T[dst][:, lo:hi], T.pad[:, :].indirect(T[kn][:, lo // 16:hi // 16]), T[src][:, slo:slo + hi - lo], A.add,
+           [al("pad"), (kn, lo // 16, hi // 16), (src, slo, slo + hi - lo)], [(dst, lo, hi)])
+
+    halves = ((CAP, A1, "psA"), (A1, V0, "psB"))
     for h in range(1, H):
         last = h == H - 1
         st = 1.0 if last else -1.0
         src = "d" if last else "n"
-        Rn, wp = "R%d" % (h - 1), "win%d" % (h - 1)
+        Rn, kn = "R%d" % (h - 1), "kn%d" % (h - 1)
         R = T[Rn]
-        o = DUMP + CAP * rank
-        keys(wp, o, o + CAP, 0)
-        by_vector(wp, o, 0, CAP)
-        act(R[:, 0:CAP], T.n[:, 0:CAP], F.Identity, 0.0, 1.0, [("n", 0, CAP)], [(Rn, 0, CAP)])
-        fold(0, CAP, last)
-        count["ar%d" % (h - 1)] = 4 * len(peers)
-        log.append((Rn, CAP, S, True, "dma", ("ar%d" % (h - 1), 4 * len(peers), {})))
-        keys(Rn, CAP, S, KB)
+        w, ws, wc = "win%d" % h, "ws%d" % h, "wc%d" % h
+        own, olo = ("win0", DUMP) if h == 1 else ("wc%d" % (h - 1), 0)
+        keys("psB", own, olo, CAP, 0, kn)
+        by_vector(kn, own, olo, Rn, 0, CAP)
+        fold(Rn, 0, CAP, last)
+        if h == 1:
+            fill(T.win2[:, DUMP:], 0.0, [al("win2")])
+        for lo, hi, ps in halves:
+            add_up(ps, [("I", Rn, lo, hi)], True, False)
         mm([(T.psD[:, 0:96], T.Z[:], R[:, CAP:CAP + 96], True, False)] + to_list("psD", 0, "W0", Rn, 0, V0, False, False),
            [al("Z"), al("W0"), al(Rn)], [al("psD")])
-        mm([(T.psA[:, 0:A1 - A0], T.I[:], R[:, A0:A1], True, False)], [al("I"), (Rn, A0, A1)], [al("psA")])
-        act(T.n[:, A0:V0], T.pad[:, :].indirect(T.ku[:, A0 // 16:V0 // 16]), F.Identity, 0.0, 1.0,
-            [al("pad"), ("ku", A0 // 16, V0 // 16)], [("n", A0, V0)])
-        by_vector(Rn, V0, V0, S)
+        add_up("psK", [("NI" if last else "I", Rn, OV, CAP), ("I", "t", OV, CAP)])
+        act(T.n[:, CAP:V0], T.pad[:, :].indirect(T[kn][:, CAP // 16:V0 // 16]), F.Identity, 0.0, 1.0,
+            [al("pad"), (kn, CAP // 16, V0 // 16)], [("n", CAP, V0)])
+        by_vector(kn, Rn, V0, "n", V0, S)
         mm(to_list("psD", KB, "W0", "n", CAP, S, False, True), [al("W0"), ("n", CAP, S)], [al("psD")])
-        mm([(T.psA[:, 0:A1 - A0], T.I[:], T.n[:, A0:A1], False, True)], [al("I"), ("n", A0, A1)], [al("psA")])
-        fold(V0, S, last)
-        back("psA", A0, A1, 1.0, src, -st, st)
+        act(T.xs[:, OV:CAP], T.psK[:, 0:CAP - OV], F.Identity, LIFT, 1.0, [al("psK")], [("xs", OV, CAP)])
+        fold("n", V0, S, last)
+        if last:
+            act(T.d[:, V0:S], T.n[:, V0:S], F.Identity, 0.0, -1.0, [("n", V0, S)], [("d", V0, S)])
+            ts(T.d[:, 0:OV], R[:, 0:OV], -1.0, None, A.mult, None, [(Rn, 0, OV)], [("d", 0, OV)])
+        for lo, hi, ps in halves:
+            add_up(ps, [("I", "n", lo, hi)], False, True)
+            act(T.sg[:, lo:hi], T[ps][:, 0:hi - lo], F.Sign, 0.5, 1.0, [al(ps)], [("sg", lo, hi)])
 
-        def second(R=R, Rn=Rn, src=src, st=st):
-            mm([(T.psB[:, 0:V0 - A1], T.I[:], R[:, A1:V0], True, False),
-                (T.psB[:, 0:V0 - A1], T.I[:], T.n[:, A1:V0], False, True)],
-               [al("I"), (Rn, A1, V0), ("n", A1, V0)], [al("psB")])
-            back("psB", A1, V0, 1.0, src, -st, st)
-        places(96, -1.0, KB * rank, second)
-        for lo in (2 * DUMP, 0, DUMP):
-            scatter(h, src, lo, lo + DUMP)
-        sent = send(h)
+        def finish(Rn=Rn):
+            for lo, hi, ps in halves:
+                add_up(ps, [("I", Rn, lo, hi), ("I", "n", lo, hi), ("J", "sg", lo, hi)])
+        places(96, -1.0, 255.0, KB * rank, finish)
+        for (lo, hi, ps), first in zip(halves, (OV, A1)):
+            act(T.xs[:, lo:hi], T[ps][:, 0:hi - lo], F.Identity, LIFT + 128.0 * st, -st, [al(ps)], [("xs", lo, hi)])
+            act(T[ws][:, :].indirect(T.pu[:, first // 16:hi // 16]), T.xs[:, first:hi], F.Silu, None, None,
+                [("xs", first, hi), ("pu", first // 16, hi // 16)], [al(ws)])
+        for lo, hi in ((V0, V1), (V1, S), (0, OV)):
+            scatter(h, Rn if lo == 0 and not last else src, lo, hi)
+        blocks = [(q - rank) % N for q in far + near + [rank]]
+        for j in blocks:
+            add_up("psP%d" % j, [("I", "CL", 0, CAP)], True, False)
+        for j in blocks:
+            mm([(T["psP%d" % j][:, 0:CAP], T.I[:], T[w][:, DUMP + CAP * j:DUMP + CAP * (j + 1)], False, True)],
+               [al("I"), al(w)], [al("psP%d" % j)])
 
-    wl, Rl = "win%d" % (H - 1), T["R%d" % (H - 1)]
+        def merge(j, ws=ws, wc=wc):
+            tt(T[wc][:, CAP * j:CAP * (j + 1)], T["psP%d" % j][:, 0:CAP], T[ws][:, DUMP + CAP * j:DUMP + CAP * (j + 1)], A.add,
+               [al("psP%d" % j), al(ws)], [(wc, CAP * j, CAP * (j + 1))])
+        for j in blocks[:len(far)]:
+            merge(j)
+        if last:
+            send(h, wc, 0, far)
+        for j in blocks[len(far):-1]:
+            merge(j)
+        send(h, wc, 0, near if last else peers)
+        merge(0)
+        if not last:
+            send_keys(h, wc, CAP)
 
-    def store(qn, q, after=()):
+    Rl = T["R%d" % (H - 1)]
+
+    def store(qn, q):
         lo, hi = CAP * q, CAP * (q + 1)
-        tok = op(qn, lambda: Q[qn].dma_start(T.y[:, lo:hi], T.yf[:, lo:hi]), [("yf", lo, hi)], (), sem="st%d" % q, inc=16, after=after)
-        return qn, tok
+        return qn, op(qn, lambda: Q[qn].dma_start(T.y[:, lo:hi], T.yf[:, lo:hi]), [("yf", lo, hi)], (), sem="st%d" % q, inc=16)
 
     lo = CAP * rank
-    act(T.yf[:, lo:lo + CAP], T[wl][:, DUMP + lo:DUMP + lo + CAP], F.Identity, 0.0, 1.0, [al(wl)], [("yf", lo, lo + CAP)])
-    stores = [store("s", rank, [sent])]
+    act(T.yf[:, lo:lo + CAP], T.wc2[:, 0:CAP], F.Relu, -1.0, 1.0, [("wc2", 0, CAP)], [("yf", lo, lo + CAP)])
+    stores = [store("s", rank)]
     for q in peers:
-        count["al%d" % q] = 4
-        log.append(("Rl", CAP * q, CAP * (q + 1), True, "dma", ("al%d" % q, 4, {})))
-    order = sorted(peers, key=lambda q: topo.die(T.cores[q]) != topo.die(core))
+        count["al%d" % q] = len(lanes(q, True))
+        log.append(("Rl", CAP * q, CAP * (q + 1), True, "dma", ("al%d" % q, count["al%d" % q], {})))
+    order = near + far
 
     def widen(qn, lo, hi):
         if qn == "v":
-            cpy(T.yf[:, lo:hi], Rl[:, lo:hi], [("Rl", lo, hi)], [("yf", lo, hi)])
+            ts(T.yf[:, lo:hi], Rl[:, lo:hi], -1.0, 0.0, A.add, A.max, [("Rl", lo, hi)], [("yf", lo, hi)])
         else:
-            act(T.yf[:, lo:hi], Rl[:, lo:hi], F.Identity, 0.0, 1.0, [("Rl", lo, hi)], [("yf", lo, hi)])
+            act(T.yf[:, lo:hi], Rl[:, lo:hi], F.Relu, -1.0, 1.0, [("Rl", lo, hi)], [("yf", lo, hi)])
     for q in order:
         widen("v", CAP * q, CAP * q + CAP // 2)
         widen("a", CAP * q + CAP // 2, CAP * (q + 1))

@@ -8,14 +8,15 @@ BIG = 2048
 EMPTY = -1024
 KB = CAP // 16
 LIFT = 288.0
+F1, AS = 128, 128
 XV = 320
-OV, A1, V0, V1 = 224, 576, 960, 1248
+OV, A1, V0, V1 = 192, 576, 960, 1248
 
 bf, f16, f32, i32, u16 = "bfloat16", "float16", "float32", "int32", "uint16"
 SCRATCH = {
     "pad": ("sbuf", [128, P + 16], bf), "cel": ("sbuf", [128, C], bf), "fi": ("sbuf", [128, 64], i32),
     "cp": ("sbuf", [128, 512], bf), "c0": ("sbuf", [8, C], bf), "c1": ("sbuf", [128, XV], bf),
-    "one": ("sbuf", [128, 144], bf), "X": ("sbuf", [128, 144], f32), "Dio": ("sbuf", [128, 128], f32),
+    "one": ("sbuf", [128, 480], bf), "X": ("sbuf", [128, 144], f32), "Dio": ("sbuf", [128, 128], f32),
     "pk": ("sbuf", [128, 1], i32), "si": ("sbuf", [128, 1], i32),
     "kf": ("sbuf", [128, 1], f32), "sf": ("sbuf", [128, 1], f32),
     "c15": ("sbuf", [128, 1], f32), "w0": ("sbuf", [128, 1], f32), "wa": ("sbuf", [128, 1], f32),
@@ -40,7 +41,7 @@ for _h in range(H):
     SCRATCH["win%d" % _h] = ("sbuf", [128, DUMP + S], bf)
     SCRATCH["R%d" % _h] = ("sbuf", [128, S], bf)
 for _h in range(H - 1):
-    SCRATCH["ko%d" % _h] = ("sbuf", [128, (N - 1) * KB], u16)
+    SCRATCH["ko%d" % _h] = ("sbuf", [128, N * KB], u16)
     SCRATCH["kn%d" % _h] = ("sbuf", [128, N * KB], u16)
     SCRATCH["ws%d" % (_h + 1)] = ("sbuf", [128, DUMP + S], f32)
     SCRATCH["wc%d" % (_h + 1)] = ("sbuf", [128, S], bf)
@@ -162,7 +163,7 @@ def rank_program(g, core, T, topo):
     iota(T.pk[:], [[0, 1]], 0, 1, [al("pk")], False)
     iota(T.X[:], [[1, 144]], 0, 0, [al("X")])
     iota(T.kf[:], [[0, 1]], 15, 1, [al("kf")])
-    select(T.W8[:], T.one[0:8, :], [[1, 144]], A.is_equal, 0.0, -15, -16, [al("one")], [al("W8")])
+    select(T.W8[:], T.one[0:8, 0:144], [[1, 144]], A.is_equal, 0.0, -15, -16, [al("one")], [al("W8")])
     select(T.ta[:], T.one[:, 0:128], ngrp, A.is_ge, 0.0, 0, 1, [al("one")], [al("ta")])
     select(T.tc[:], T.one[:, 0:128], grp, A.is_ge, 0.0, 15, -1, [al("one")], [al("tc")])
     select(T.td[:], T.ta[:], col, A.is_gt, 0.0, 0, -1, [al("ta")], [al("td")])
@@ -171,12 +172,13 @@ def rank_program(g, core, T, topo):
     select(T.I[:], T.one[:, 0:128], col, A.is_equal, 0.0, 0, -1, [al("one")], [al("I")])
     select(T.L[:], T.td[:], col, A.not_equal, float(BIG), 0, -1, [al("td")], [al("L")])
     select(T.U[:], T.te[:], col, A.not_equal, float(1 - BIG), 0, -1, [al("te")], [al("U")])
-    iota(T.m5[:], [[0, 96], [4096, 5]], 0, 0, [al("m5")])
-    iota(T.win1[:, DUMP:], [[0, S]], 0, 0, [al("win1")])
+    iota(T.ws2[:, DUMP:DUMP + 768], [[0, 768]], int(LIFT), 0, [("ws2", DUMP, DUMP + 768)])
+    act(T.m5[:], T.one[:, 0:480], F.Identity, 0.0, 4096.0, [al("one")], [al("m5")])
+    act(T.m5[:, 0:480:5], T.one[:, 0:96], F.Identity, 0.0, 0.0, [al("one")], [al("m5")])
 
     ts(T.si[:], T.pk[:], 15, None, A.bitwise_and, None, [al("pk")], [al("si")])
     cpy(T.sf[:], T.si[:], [al("si")], [al("sf")])
-    fill(T.win0[:, DUMP:], 0.0, [al("win0")])
+    fill(T.win0[:, DUMP:DUMP + 768], 0.0, [("win0", DUMP, DUMP + 768)])
     ts(T.I16[:], T.X[:, 0:16], T.sf[:], None, A.is_equal, None, [al("X"), al("sf")], [al("I16")])
 
     ts(T.la[:, 0:64], T.fi[:], 511, None, A.bitwise_and, None, [al("fi")], [al("la")])
@@ -187,10 +189,12 @@ def rank_program(g, core, T, topo):
     cpy(T.ku[:], T.fi[:], [al("fi")], [al("ku")])
     ts(T.W1[:], T.X[:], T.c15[:], -1.0, A.is_equal, A.mult, [al("X"), al("c15")], [al("W1")])
     fill(T.pad[:, P:P + 16], float(EMPTY), [("pad", P, P + 16)])
+    ts(T.w0[:], T.sf[:], 0.0, -1.0, A.is_equal, A.mult, [al("sf")], [al("w0")])
     for a in range(4):
         act(T.G[:, 256 * a:256 * a + 256], T.cp[:, :].indirect(T.lu[:, 16 * a:16 * a + 16]), F.Identity, 0.0, 1.0,
             [al("cp"), al("lu")], [("G", 256 * a, 256 * a + 256)])
     act(T.c1[:], T.cel[:, 0:XV], F.Identity, 1.0, 1.0, [("cel", 0, XV)], [al("c1")])
+    act(T.win0[:, DUMP + 768:], T.G[:, 0:768], F.Identity, 0.0, 0.0, [al("G")], [("win0", DUMP + 768, DUMP + S)])
     mm([(T.psD[:, 0:64], T.W8[:, 15 - r:143 - r], T.c0[:, r:C:16], r == 0, False) for r in range(16)],
        [al("W8"), al("c0")], [al("psD")])
     for a in range(4):
@@ -220,9 +224,9 @@ def rank_program(g, core, T, topo):
         for q in range(N):
             op("v", lambda q=q: V.tensor_tensor_scan(T.P5[:, q + 1:5 * k:5], T["psP%d" % q][:, 0:k], T.m5[:, 4:5 * k:5],
                                                     float(DUMP - BIG + CAP * ((q - rank) % N)), A.add, A.min),
-               [al("psP%d" % q), al("m5")], [("P5", q + 1, q + 2)])
+               [al("psP%d" % q), ("m5", 0, 5 * k)], [("P5", q + 1, q + 2)])
         op("v", lambda: V.tensor_tensor_scan(T.M5[:, 0:5 * k], T.m5[:, 0:5 * k], T.P5[:, 0:5 * k], 0.0, A.min, A.max),
-           [al("m5"), al("P5")], [al("M5")])
+           [("m5", 0, 5 * k), al("P5")], [al("M5")])
         for (x, c, m) in parts:
             cpy(T.pu[:, x:x + m], T.M5[:, 5 * c + 4:5 * (c + m):5], [al("M5")], [("pu", x, x + m)])
 
@@ -237,9 +241,13 @@ def rank_program(g, core, T, topo):
     peers = [q for q in range(N) if q != rank]
     far = [q for q in peers if topo.die(T.cores[q]) != topo.die(core)]
     near = [q for q in peers if q not in far]
+    if near[0] < rank:
+        far = far[::-1]
 
     def lanes(q, wide):
         eng = topo.engines(core, T.cores[q])
+        if wide == 2:
+            return eng
         if q in far:
             return eng[0::2][4 * far.index(q):4 * far.index(q) + 4]
         return eng[1::2][0:8 if wide else 4]
@@ -257,10 +265,13 @@ def rank_program(g, core, T, topo):
 
     def send(h, w, off, to):
         last = h == H - 1
-        need("g", [k[5] for k in log if k[0] == w and k[3]][-1])
+        for q in to:
+            lo = off + CAP * ((q - rank) % N)
+            for k in [k for k in log if k[0] == w and k[3] and k[1] < lo + CAP and lo < k[2]][::-1]:
+                need("g", k[5])
         tot = fused(to, lambda j: T[w][:, off + CAP * j:off + CAP * (j + 1)], "R%d" % h, CAP,
                     "al%d" % rank if last else "ar%d" % h, "ls%d" % h,
-                    (lambda q: rank) if last else (lambda q: (rank - q) % N), h > 0)
+                    (lambda q: rank) if last else (lambda q: (rank - q) % N), h)
         if not last:
             count["ar%d" % h] = tot
             log.append(("R%d" % h, CAP, S, True, "dma", ("ar%d" % h, tot, {})))
@@ -271,12 +282,12 @@ def rank_program(g, core, T, topo):
         ts(T.li[:, c0:c0 + k], T[ps][:, 0:k], -257.0, None, A.add, None, [al(ps)], [("li", c0, c0 + k)])
         ts(T.la[:, c0:c0 + k], T.li[:, c0:c0 + k], (P - 1) | (1 << 17), None, A.bitwise_and, None,
            [("li", c0, c0 + k)], [("la", c0, c0 + k)])
-        return ts(T[dst][:, 0:k], T.la[:, c0:c0 + k], float(P), None, A.min, None, [("la", c0, c0 + k)], [(dst, 0, k)])
+        return ts(T[dst][:, c0:c0 + k], T.la[:, c0:c0 + k], float(P), None, A.min, None, [("la", c0, c0 + k)], [(dst, c0, c0 + k)])
 
-    def send_keys(h, src, lo):
+    def send_keys(h, src, lo, c0):
         ko, kn = "ko%d" % h, "kn%d" % h
-        need("g", keys("psK", src, lo, S - CAP, KB, ko))
-        tot = fused(peers, lambda j: T[ko][:, KB * (j - 1):KB * j], kn, KB, "ak%d" % h, "lk%d" % h, lambda q: (rank - q) % N, h > 0)
+        need("g", keys("psK", src, lo + 16 * c0, S - 16 * c0, c0, ko))
+        tot = fused(peers, lambda j: T[ko][:, KB * j:KB * (j + 1)], kn, KB, "ak%d" % h, "lk%d" % h, lambda q: (rank - q) % N, h > 0)
         count["ak%d" % h] = tot
         log.append((kn, KB, N * KB, True, "dma", ("ak%d" % h, tot, {})))
 
@@ -306,16 +317,16 @@ def rank_program(g, core, T, topo):
     for lo, hi in ((0, DUMP), (DUMP, C)):
         scatter(0, "n", lo, hi)
     act(T.Wk[:], T.W1[:], F.Identity, 0.0, T.wk[:], [al("W1"), al("wk")], [al("Wk")])
-    ts(T.w0[:], T.sf[:], 0.0, -1.0, A.is_equal, A.mult, [al("sf")], [al("w0")])
-    fill(T.Z[:], 0.0, [al("Z")])
+    act(T.Z[:], T.I[:], F.Identity, 0.0, 0.0, [al("I")], [al("Z")])
     act(T.W0[:], T.W1[:], F.Identity, 0.0, T.w0[:], [al("W1"), al("w0")], [al("W0")])
     act(T.J[:], T.I[:], F.Identity, 0.0, -128.0, [al("I")], [al("J")])
-    act(T.NI[:], T.I[:], F.Identity, 0.0, -1.0, [al("I")], [al("NI")])
     act(T.CL[:], T.pad[:, 0:CAP], F.Identity, -LIFT, 0.0, [al("pad")], [al("CL")])
     act(T.ws1[:, DUMP:], T.pad[:, 0:S], F.Silu, LIFT, 0.0, [al("pad")], [al("ws1")])
     send(0, "win0", DUMP, peers)
-    send_keys(0, "win0", DUMP + CAP)
-    iota(T.ws2[:, DUMP:], [[0, S]], int(LIFT), 0, [al("ws2")])
+    fill(T.win1[:, DUMP:], 0.0, [al("win1")])
+    send_keys(0, "win0", DUMP, 0)
+    iota(T.ws2[:, DUMP + 768:], [[0, S - 768]], int(LIFT), 0, [("ws2", DUMP + 768, DUMP + S)])
+    iota(T.win2[:, DUMP:], [[0, S]], 0, 0, [al("win2")])
 
     def by_vector(kn, src, slo, dst, lo, hi):
         tt(T[dst][:, lo:hi], T.pad[:, :].indirect(T[kn][:, lo // 16:hi // 16]), T[src][:, slo:slo + hi - lo], A.add,
@@ -330,22 +341,20 @@ def rank_program(g, core, T, topo):
         R = T[Rn]
         w, ws, wc = "win%d" % h, "ws%d" % h, "wc%d" % h
         own, olo = ("win0", DUMP) if h == 1 else ("wc%d" % (h - 1), 0)
-        keys("psB", own, olo, CAP, 0, kn)
-        by_vector(kn, own, olo, Rn, 0, CAP)
-        fold(Rn, 0, CAP, last)
-        if h == 1:
-            fill(T.win2[:, DUMP:], 0.0, [al("win2")])
+        by_vector("ko%d" % (h - 1), own, olo, Rn, 0, CAP)
+        add_up("psD", [("Z", "CL", 0, 96)], True, False)
         for lo, hi, ps in halves:
             add_up(ps, [("I", Rn, lo, hi)], True, False)
-        mm([(T.psD[:, 0:96], T.Z[:], R[:, CAP:CAP + 96], True, False)] + to_list("psD", 0, "W0", Rn, 0, V0, False, False),
-           [al("Z"), al("W0"), al(Rn)], [al("psD")])
-        add_up("psK", [("NI" if last else "I", Rn, OV, CAP), ("I", "t", OV, CAP)])
+        mm(to_list("psD", 0, "W0", Rn, 0, V0, False, False), [al("W0"), al(Rn)], [al("psD")])
         act(T.n[:, CAP:V0], T.pad[:, :].indirect(T[kn][:, CAP // 16:V0 // 16]), F.Identity, 0.0, 1.0,
             [al("pad"), (kn, CAP // 16, V0 // 16)], [("n", CAP, V0)])
         by_vector(kn, Rn, V0, "n", V0, S)
         mm(to_list("psD", KB, "W0", "n", CAP, S, False, True), [al("W0"), ("n", CAP, S)], [al("psD")])
-        act(T.xs[:, OV:CAP], T.psK[:, 0:CAP - OV], F.Identity, LIFT, 1.0, [al("psK")], [("xs", OV, CAP)])
+        fold(Rn, 0, CAP, last)
+        act(T.sg[:, OV:CAP], T.t[:, OV:CAP], F.Identity, LIFT, 1.0, [("t", OV, CAP)], [("sg", OV, CAP)])
         fold("n", V0, S, last)
+        tt(T.xs[:, OV:CAP], T.sg[:, OV:CAP], R[:, OV:CAP], A.subtract if last else A.add,
+           [("sg", OV, CAP), (Rn, OV, CAP)], [("xs", OV, CAP)])
         if last:
             act(T.d[:, V0:S], T.n[:, V0:S], F.Identity, 0.0, -1.0, [("n", V0, S)], [("d", V0, S)])
             ts(T.d[:, 0:OV], R[:, 0:OV], -1.0, None, A.mult, None, [(Rn, 0, OV)], [("d", 0, OV)])
@@ -363,26 +372,30 @@ def rank_program(g, core, T, topo):
                 [("xs", first, hi), ("pu", first // 16, hi // 16)], [al(ws)])
         for lo, hi in ((V0, V1), (V1, S), (0, OV)):
             scatter(h, Rn if lo == 0 and not last else src, lo, hi)
-        blocks = [(q - rank) % N for q in far + near + [rank]]
-        for j in blocks:
-            add_up("psP%d" % j, [("I", "CL", 0, CAP)], True, False)
-        for j in blocks:
-            mm([(T["psP%d" % j][:, 0:CAP], T.I[:], T[w][:, DUMP + CAP * j:DUMP + CAP * (j + 1)], False, True)],
-               [al("I"), al(w)], [al("psP%d" % j)])
-
-        def merge(j, ws=ws, wc=wc):
-            tt(T[wc][:, CAP * j:CAP * (j + 1)], T["psP%d" % j][:, 0:CAP], T[ws][:, DUMP + CAP * j:DUMP + CAP * (j + 1)], A.add,
-               [al("psP%d" % j), al(ws)], [(wc, CAP * j, CAP * (j + 1))])
-        for j in blocks[:len(far)]:
-            merge(j)
-        if last:
-            send(h, wc, 0, far)
-        for j in blocks[len(far):-1]:
-            merge(j)
-        send(h, wc, 0, near if last else peers)
-        merge(0)
+        b1, b2, b3 = [CAP * ((q - rank) % N) for q in far + near]
+        by_pe = [(b1, b1 + F1, "psA"), (b1 + F1, b1 + CAP, "psP0"), (b2, b2 + CAP, "psP1")]
+        by_act = [(b3, b3 + CAP, "psP2")] if last else [(b3 + AS, b3 + CAP, "psP2"), (0, CAP, "psP3")]
+        a0, a1 = (0, CAP) if last else (b3, b3 + AS)
+        for lo, hi, ps in by_pe:
+            add_up(ps, [("I", "CL", 0, hi - lo)], True, False)
+        for lo, hi, ps in by_pe:
+            add_up(ps, [("I", w, DUMP + lo, DUMP + hi)], False, True)
+        act(T.sg[:, a0:a1], T[ws][:, DUMP + a0:DUMP + a1], F.Identity, -LIFT, 1.0, [al(ws)], [("sg", a0, a1)])
+        add_up("psK", [("I", w, DUMP + a0, DUMP + a1), ("I", "sg", a0, a1)])
+        for i, (lo, hi, ps) in enumerate(by_act):
+            act(T[ps][:, 0:hi - lo], T[ws][:, DUMP + lo:DUMP + hi], F.Identity, -LIFT, 1.0, [al(ws)], [al(ps)])
+            if i == 0 and not last:
+                act(T[wc][:, a0:a1], T.psK[:, 0:AS], F.Identity, 0.0, 1.0, [al("psK")], [(wc, a0, a1)])
+        for i, (lo, hi, ps) in enumerate(by_pe + by_act):
+            o = ws if i < len(by_pe) else w
+            tt(T[wc][:, lo:hi], T[ps][:, 0:hi - lo], T[o][:, DUMP + lo:DUMP + hi], A.add, [al(ps), al(o)], [(wc, lo, hi)])
+            if last and 0 < i < len(by_pe):
+                send(h, wc, 0, [far[i - 1]])
+            if i == len(by_pe):
+                send(h, wc, 0, near if last else peers)
         if not last:
-            send_keys(h, wc, CAP)
+            send_keys(h, wc, 0, KB)
+            keys("psB", wc, 0, CAP, 0, "ko%d" % h)
 
     Rl = T["R%d" % (H - 1)]
 
@@ -391,12 +404,12 @@ def rank_program(g, core, T, topo):
         return qn, op(qn, lambda: Q[qn].dma_start(T.y[:, lo:hi], T.yf[:, lo:hi]), [("yf", lo, hi)], (), sem="st%d" % q, inc=16)
 
     lo = CAP * rank
-    act(T.yf[:, lo:lo + CAP], T.wc2[:, 0:CAP], F.Relu, -1.0, 1.0, [("wc2", 0, CAP)], [("yf", lo, lo + CAP)])
+    act(T.yf[:, lo:lo + CAP], T.psK[:, 0:CAP], F.Relu, -1.0, 1.0, [al("psK")], [("yf", lo, lo + CAP)])
     stores = [store("s", rank)]
     for q in peers:
-        count["al%d" % q] = len(lanes(q, True))
+        count["al%d" % q] = len(lanes(q, 2))
         log.append(("Rl", CAP * q, CAP * (q + 1), True, "dma", ("al%d" % q, count["al%d" % q], {})))
-    order = near + far
+    order = far + near
 
     def widen(qn, lo, hi):
         if qn == "v":

from concourse.bass import DstId, RemoteDMATransfer
from concourse.mybir import AluOpType as A, ActivationFunctionType as F

N, C, CAP, P, H = 4, 1024, 384, 8192, 3
S = N * CAP
DUMP = 512
BIG = 2048
EMPTY = -1024
KB = CAP // 16
LIFT = 288.0
F1, AS = 128, 128
XV = 320
OV, A1, V0, V1 = 192, 576, 960, 1248

bf, f16, f32, i32, u16 = "bfloat16", "float16", "float32", "int32", "uint16"
SCRATCH = {
    "pad": ("sbuf", [128, P + 16], bf), "cel": ("sbuf", [128, C], bf), "fi": ("sbuf", [128, 64], i32),
    "cp": ("sbuf", [128, 512], bf), "c0": ("sbuf", [8, C], bf), "c1": ("sbuf", [128, XV], bf),
    "one": ("sbuf", [128, 480], bf), "X": ("sbuf", [128, 144], f32), "Dio": ("sbuf", [128, 128], f32),
    "pk": ("sbuf", [128, 1], i32), "si": ("sbuf", [128, 1], i32),
    "kf": ("sbuf", [128, 1], f32), "sf": ("sbuf", [128, 1], f32),
    "c15": ("sbuf", [128, 1], f32), "w0": ("sbuf", [128, 1], f32), "wa": ("sbuf", [128, 1], f32),
    "wb": ("sbuf", [128, 1], f32), "wk": ("sbuf", [128, 1], f32),
    "W0": ("sbuf", [128, 144], bf), "W1": ("sbuf", [128, 144], bf), "Wk": ("sbuf", [128, 144], bf), "W8": ("sbuf", [8, 144], bf),
    "I": ("sbuf", [128, 128], bf), "J": ("sbuf", [128, 128], bf), "NI": ("sbuf", [128, 128], bf),
    "I16": ("sbuf", [128, 16], bf), "Z": ("sbuf", [128, 128], bf), "CL": ("sbuf", [128, CAP], bf),
    "ta": ("sbuf", [128, 128], bf), "tc": ("sbuf", [128, 128], bf), "td": ("sbuf", [128, 128], bf), "te": ("sbuf", [128, 128], bf),
    "L": ("sbuf", [128, 128], f16), "U": ("sbuf", [128, 128], f16),
    "m5": ("sbuf", [128, 480], bf), "P5": ("sbuf", [128, 480], f16), "M5": ("sbuf", [128, 480], f16),
    "E": ("sbuf", [128, 384], f16),
    "li": ("sbuf", [128, 96], i32), "la": ("sbuf", [128, 96], i32), "lb": ("sbuf", [128, 96], i32),
    "ku": ("sbuf", [128, 64], u16), "lu": ("sbuf", [128, 64], u16), "hu": ("sbuf", [128, 64], u16),
    "pu": ("sbuf", [128, 96], u16),
    "G": ("sbuf", [128, C], bf), "Sel": ("sbuf", [128, C], bf),
    "n": ("sbuf", [128, S], bf), "t": ("sbuf", [128, S], bf), "d": ("sbuf", [128, S], bf), "sg": ("sbuf", [128, S], bf),
    "xs": ("sbuf", [128, S], f32), "yf": ("sbuf", [128, S], f32),
    "psK": ("psum", [128, 512], f32), "psD": ("psum", [128, 512], f32),
    "psA": ("psum", [128, 512], f32), "psB": ("psum", [128, 512], f32),
}
for _h in range(H):
    SCRATCH["win%d" % _h] = ("sbuf", [128, DUMP + S], bf)
    SCRATCH["R%d" % _h] = ("sbuf", [128, S], bf)
for _h in range(H - 1):
    SCRATCH["ko%d" % _h] = ("sbuf", [128, N * KB], u16)
    SCRATCH["kn%d" % _h] = ("sbuf", [128, N * KB], u16)
    SCRATCH["ws%d" % (_h + 1)] = ("sbuf", [128, DUMP + S], f32)
    SCRATCH["wc%d" % (_h + 1)] = ("sbuf", [128, S], bf)
for _q in range(N):
    SCRATCH["psP%d" % _q] = ("psum", [128, 512], f32)

SEMAPHORES = (["cv", "ca", "cp", "cg", "dfi", "dcp", "dc0", "dcel", "dcem", "dpad", "ar0", "ar1", "ak0", "ak1",
               "ls0", "ls1", "ls2", "lk0", "lk1"]
              + ["al%d" % q for q in range(N)] + ["st%d" % q for q in range(N)])


def rank_program(g, core, T, topo):
    rank = T.rank_of(core)
    if rank is None:
        return
    Q = {"v": g.vector, "a": g.scalar, "p": g.tensor, "g": g, "s": g.sync}
    OWN = {"v": "cv", "a": "ca", "p": "cp", "g": "cg"}
    known = {q: {} for q in Q}
    count = {}
    waited = {}
    log = []

    def need(q, tok):
        sem, val, clock = tok
        if known[q].get(sem, 0) < val:
            Q[q].wait_ge(T.sem[sem], val)
            waited[sem] = max(waited.get(sem, 0), val)
        for s_, v_ in list(clock.items()) + [(sem, val)]:
            if known[q].get(s_, 0) < v_:
                known[q][s_] = v_

    def op(q, fn, r=(), w=(), sem=None, inc=1):
        eng = q if sem is None else "dma"
        toks = []
        for acc, wr in [(x, False) for x in r] + [(x, True) for x in w]:
            for (b, lo, hi, owr, oq, tok) in log:
                if b != acc[0] or hi <= acc[1] or acc[2] <= lo:
                    continue
                same = oq == eng and eng != "dma"
                if same and q == "p":
                    continue
                if wr or owr or (b.startswith("ps") and not same):
                    toks.append(tok)
        best = {}
        for tok in toks:
            if tok[0] not in best or best[tok[0]][1] < tok[1]:
                best[tok[0]] = tok
        for tok in sorted(best.values(), key=lambda k: -len(k[2])):
            need(q, tok)
        ins = fn()
        s_ = OWN[q] if sem is None else sem
        count[s_] = count.get(s_, 0) + inc
        ins.then_inc(T.sem[s_], inc)
        tok = (s_, count[s_], dict(known[q]))
        for acc, wr in [(x, False) for x in r] + [(x, True) for x in w]:
            log.append((acc[0], acc[1], acc[2], wr, eng, tok))
        return tok

    def al(b):
        return (b, 0, 1 << 20)

    V, ACT, PE = g.vector, g.scalar, g.tensor

    def ts(out, in0, s1, s2, o0, o1, r, w):
        if o1 is None:
            return op("v", lambda: V.tensor_scalar(out, in0, s1, None, o0), r, w)
        return op("v", lambda: V.tensor_scalar(out, in0, s1, s2, o0, o1), r, w)

    def tt(out, in0, in1, o, r, w):
        return op("v", lambda: V.tensor_tensor(out, in0, in1, o), r, w)

    def cpy(out, in_, r, w):
        return op("v", lambda: V.tensor_copy(out, in_), r, w)

    def fill(out, value, w):
        return op("v", lambda: V.memset(out, value), (), w)

    def act(out, in_, func, bias, scale, r, w):
        if bias is None:
            return op("a", lambda: ACT.activation(out, in_, func), r, w)
        return op("a", lambda: ACT.activation(out, in_, func, bias=bias, scale=scale), r, w)

    def iota(out, pattern, base, cm, w, flag=True):
        if flag:
            return op("g", lambda: g.iota(out, pattern, base, cm, allow_small_or_imprecise_dtypes=True), (), w)
        return op("g", lambda: g.iota(out, pattern, base, cm), (), w)

    def select(out, in_, pattern, cmp, other, base, cm, r, w):
        return op("g", lambda: g.affine_select(out, in_, pattern, cmp, other, base, cm), r, w)

    def mm(calls, r, w):
        def run():
            ins = None
            for (o, l, x, st, sp) in calls:
                ins = PE.matmul(o, l, x, st, sp)
            return ins
        return op("p", run, r, w)

    def add_up(ps, terms, start=True, stop=True):
        mm([(T[ps][:, 0:hi - lo], T[wt][:], T[b][:, lo:hi], start and i == 0, stop and i == len(terms) - 1)
            for i, (wt, b, lo, hi) in enumerate(terms)],
           [al(wt) for (wt, b, lo, hi) in terms] + [(b, lo, hi) for (wt, b, lo, hi) in terms], [al(ps)])

    def to_list(ps, c0, W, src, lo, hi, start, stop):
        k = (hi - lo) // 16
        return [(T[ps][:, c0:c0 + k], T[W][:, 15 - r:143 - r], T[src][:, lo + r:hi:16], start and r == 0, stop and r == 15)
                for r in range(16)]

    op("s", lambda: g.sync.dma_start(T.fi[:], T.first[:]), (), [al("fi")], sem="dfi", inc=16)
    op("a", lambda: g.scalar.dma_start(T.cp[:], T.pads[0:128:16, :]), (), [al("cp")], sem="dcp", inc=16)
    op("a", lambda: g.scalar.dma_start(T.c0[:], T.cells[0:128:16, :]), (), [al("c0")], sem="dc0", inc=16)
    op("s", lambda: g.sync.dma_start(T.cel[:, 0:XV], T.cells[:, 0:XV]), (), [("cel", 0, XV)], sem="dcel", inc=16)
    op("s", lambda: g.sync.dma_start(T.pad[:, 0:P], T.pads[:]), (), [("pad", 0, P)], sem="dpad", inc=16)
    op("s", lambda: g.sync.dma_start(T.cel[:, XV:C], T.cells[:, XV:C]), (), [("cel", XV, C)], sem="dcem", inc=16)

    col, grp = [[1, 128]], [[16, 8], [0, 16]]
    ncol, ngrp = [[-1, 128]], [[-16, 8], [0, 16]]
    fill(T.one[:], 1.0, [al("one")])
    iota(T.pk[:], [[0, 1]], 0, 1, [al("pk")], False)
    iota(T.X[:], [[1, 144]], 0, 0, [al("X")])
    iota(T.kf[:], [[0, 1]], 15, 1, [al("kf")])
    select(T.W8[:], T.one[0:8, 0:144], [[1, 144]], A.is_equal, 0.0, -15, -16, [al("one")], [al("W8")])
    select(T.ta[:], T.one[:, 0:128], ngrp, A.is_ge, 0.0, 0, 1, [al("one")], [al("ta")])
    select(T.tc[:], T.one[:, 0:128], grp, A.is_ge, 0.0, 15, -1, [al("one")], [al("tc")])
    select(T.td[:], T.ta[:], col, A.is_gt, 0.0, 0, -1, [al("ta")], [al("td")])
    select(T.te[:], T.tc[:], ncol, A.is_gt, 0.0, 0, 1, [al("tc")], [al("te")])
    iota(T.Dio[:], [[0, 4], [16, 32]], 0, 0, [al("Dio")])
    select(T.I[:], T.one[:, 0:128], col, A.is_equal, 0.0, 0, -1, [al("one")], [al("I")])
    select(T.L[:], T.td[:], col, A.not_equal, float(BIG), 0, -1, [al("td")], [al("L")])
    select(T.U[:], T.te[:], col, A.not_equal, float(1 - BIG), 0, -1, [al("te")], [al("U")])
    iota(T.ws2[:, DUMP:DUMP + 768], [[0, 768]], int(LIFT), 0, [("ws2", DUMP, DUMP + 768)])
    act(T.m5[:], T.one[:, 0:480], F.Identity, 0.0, 4096.0, [al("one")], [al("m5")])
    act(T.m5[:, 0:480:5], T.one[:, 0:96], F.Identity, 0.0, 0.0, [al("one")], [al("m5")])

    ts(T.si[:], T.pk[:], 15, None, A.bitwise_and, None, [al("pk")], [al("si")])
    cpy(T.sf[:], T.si[:], [al("si")], [al("sf")])
    fill(T.win0[:, DUMP:DUMP + 768], 0.0, [("win0", DUMP, DUMP + 768)])
    ts(T.I16[:], T.X[:, 0:16], T.sf[:], None, A.is_equal, None, [al("X"), al("sf")], [al("I16")])

    ts(T.la[:, 0:64], T.fi[:], 511, None, A.bitwise_and, None, [al("fi")], [al("la")])
    ts(T.lb[:, 0:64], T.fi[:], 9, None, A.logical_shift_right, None, [al("fi")], [al("lb")])
    cpy(T.lu[:], T.la[:, 0:64], [al("la")], [al("lu")])
    cpy(T.hu[:], T.lb[:, 0:64], [al("lb")], [al("hu")])
    ts(T.c15[:], T.kf[:], T.sf[:], None, A.subtract, None, [al("kf"), al("sf")], [al("c15")])
    cpy(T.ku[:], T.fi[:], [al("fi")], [al("ku")])
    ts(T.W1[:], T.X[:], T.c15[:], -1.0, A.is_equal, A.mult, [al("X"), al("c15")], [al("W1")])
    fill(T.pad[:, P:P + 16], float(EMPTY), [("pad", P, P + 16)])
    ts(T.w0[:], T.sf[:], 0.0, -1.0, A.is_equal, A.mult, [al("sf")], [al("w0")])
    for a in range(4):
        act(T.G[:, 256 * a:256 * a + 256], T.cp[:, :].indirect(T.lu[:, 16 * a:16 * a + 16]), F.Identity, 0.0, 1.0,
            [al("cp"), al("lu")], [("G", 256 * a, 256 * a + 256)])
    act(T.c1[:], T.cel[:, 0:XV], F.Identity, 1.0, 1.0, [("cel", 0, XV)], [al("c1")])
    act(T.win0[:, DUMP + 768:], T.G[:, 0:768], F.Identity, 0.0, 0.0, [al("G")], [("win0", DUMP + 768, DUMP + S)])
    mm([(T.psD[:, 0:64], T.W8[:, 15 - r:143 - r], T.c0[:, r:C:16], r == 0, False) for r in range(16)],
       [al("W8"), al("c0")], [al("psD")])
    for a in range(4):
        tt(T.Sel[:, 256 * a:256 * a + 256], T.I16[:, :].indirect(T.hu[:, 16 * a:16 * a + 16]), T.G[:, 256 * a:256 * a + 256],
           A.mult, [al("I16"), al("hu"), ("G", 256 * a, 256 * a + 256)], [("Sel", 256 * a, 256 * a + 256)])
    mm(to_list("psD", 0, "W1", "Sel", 0, C, False, True), [al("W1"), al("Sel")], [al("psD")])
    x0 = (-KB * rank) % 32
    ts(T.P5[:, 0:480:5], T.Dio[:, x0:x0 + 96], T.sf[:], None, A.add, None, [al("Dio"), al("sf")], [("P5", 0, 1)])
    ts(T.wa[:], T.sf[:], 1.0, None, A.is_equal, None, [al("sf")], [al("wa")])
    ts(T.wb[:], T.sf[:], 2.0, 256.0, A.is_equal, A.mult, [al("sf")], [al("wb")])
    tt(T.wk[:], T.wa[:], T.wb[:], A.add, [al("wa"), al("wb")], [al("wk")])
    tt(T.n[:, 0:XV], T.pad[:, :].indirect(T.ku[:, 0:XV // 16]), T.c1[:], A.subtract,
       [al("pad"), al("ku"), al("c1")], [("n", 0, XV)])

    def places(k, sign, base, rot, between):
        parts = [(0, rot, k - rot)] + ([(k - rot, 0, rot)] if rot else [])
        for (x, c, m) in parts:
            ts(T.li[:, c:c + m], T.psD[:, x:x + m], sign, base, A.mult, A.add, [al("psD")], [("li", c, c + m)])
        ts(T.la[:, 0:k], T.li[:, 0:k], 1027, None, A.bitwise_and, None, [al("li")], [al("la")])
        for q in range(N):
            e = ("E", 96 * q, 96 * q + 96)
            ts(T.E[:, 96 * q:96 * q + k], T.la[:, 0:k], float(q), None, A.is_equal, None, [al("la")], [e])
            ps = T["psP%d" % q]
            mm([(ps[:, 0:k], T.L[:], T.E[:, 96 * q:96 * q + k], True, False),
                (ps[:, 1:k], T.U[:], T.E[:, 96 * q:96 * q + k - 1], False, True)], [al("L"), al("U"), e], [al("psP%d" % q)])
        between()
        for q in range(N):
            op("v", lambda q=q: V.tensor_tensor_scan(T.P5[:, q + 1:5 * k:5], T["psP%d" % q][:, 0:k], T.m5[:, 4:5 * k:5],
                                                    float(DUMP - BIG + CAP * ((q - rank) % N)), A.add, A.min),
               [al("psP%d" % q), ("m5", 0, 5 * k)], [("P5", q + 1, q + 2)])
        op("v", lambda: V.tensor_tensor_scan(T.M5[:, 0:5 * k], T.m5[:, 0:5 * k], T.P5[:, 0:5 * k], 0.0, A.min, A.max),
           [("m5", 0, 5 * k), al("P5")], [al("M5")])
        for (x, c, m) in parts:
            cpy(T.pu[:, x:x + m], T.M5[:, 5 * c + 4:5 * (c + m):5], [al("M5")], [("pu", x, x + m)])

    def fold(src, lo, hi, last):
        ts(T.t[:, lo:hi], T[src][:, lo:hi], 0.0, 256.0 if last else -256.0, A.is_ge, A.mult, [(src, lo, hi)], [("t", lo, hi)])

    def scatter(h, src, lo, hi):
        w = "win%d" % h
        tt(T[w][:, :].indirect(T.pu[:, lo // 16:hi // 16]), T[src][:, lo:hi], T.t[:, lo:hi], A.add,
           [(src, lo, hi), ("t", lo, hi), ("pu", lo // 16, hi // 16)], [al(w)])

    peers = [q for q in range(N) if q != rank]
    far = [q for q in peers if topo.die(T.cores[q]) != topo.die(core)]
    near = [q for q in peers if q not in far]
    if near[0] < rank:
        far = far[::-1]

    def lanes(q, wide):
        eng = topo.engines(core, T.cores[q])
        if wide == 2:
            return eng
        if q in far:
            return eng[0::2][4 * far.index(q):4 * far.index(q) + 4]
        return eng[1::2][0:8 if wide else 4]

    def fused(to, src, dst, width, rsem, lsem, slot, wide):
        trs = []
        for q in to:
            rid, pid, _se = topo.addr(T.cores[q])
            trs.append(RemoteDMATransfer(dst_ids=[DstId(rid=rid, pnc=pid)], dma_engine_mask=sum(1 << e for e in lanes(q, wide)),
                                         remote_sem=T.sem[rsem], src=src((q - rank) % N),
                                         dst=T[dst][:, width * slot(q):width * (slot(q) + 1)]))
        g.remote_dma_fused(trs, local_sem=T.sem[lsem])
        count[lsem] = count.get(lsem, 0) + sum(len(lanes(q, wide)) for q in to)
        return count[lsem]

    def send(h, w, off, to):
        last = h == H - 1
        for q in to:
            lo = off + CAP * ((q - rank) % N)
            for k in [k for k in log if k[0] == w and k[3] and k[1] < lo + CAP and lo < k[2]][::-1]:
                need("g", k[5])
        tot = fused(to, lambda j: T[w][:, off + CAP * j:off + CAP * (j + 1)], "R%d" % h, CAP,
                    "al%d" % rank if last else "ar%d" % h, "ls%d" % h,
                    (lambda q: rank) if last else (lambda q: (rank - q) % N), h)
        if not last:
            count["ar%d" % h] = tot
            log.append(("R%d" % h, CAP, S, True, "dma", ("ar%d" % h, tot, {})))

    def keys(ps, src, lo, width, c0, dst):
        k = width // 16
        mm(to_list(ps, 0, "Wk", src, lo, lo + width, True, True), [al("Wk"), (src, lo, lo + width)], [al(ps)])
        ts(T.li[:, c0:c0 + k], T[ps][:, 0:k], -257.0, None, A.add, None, [al(ps)], [("li", c0, c0 + k)])
        ts(T.la[:, c0:c0 + k], T.li[:, c0:c0 + k], (P - 1) | (1 << 17), None, A.bitwise_and, None,
           [("li", c0, c0 + k)], [("la", c0, c0 + k)])
        return ts(T[dst][:, c0:c0 + k], T.la[:, c0:c0 + k], float(P), None, A.min, None, [("la", c0, c0 + k)], [(dst, c0, c0 + k)])

    def send_keys(h, src, lo, c0):
        ko, kn = "ko%d" % h, "kn%d" % h
        need("g", keys("psK", src, lo + 16 * c0, S - 16 * c0, c0, ko))
        tot = fused(peers, lambda j: T[ko][:, KB * j:KB * (j + 1)], kn, KB, "ak%d" % h, "lk%d" % h, lambda q: (rank - q) % N, h > 0)
        count["ak%d" % h] = tot
        log.append((kn, KB, N * KB, True, "dma", ("ak%d" % h, tot, {})))

    cuts = [(XV, XV + 256, "psA"), (XV + 256, XV + 512, "psB"), (XV + 512, C, "psK")]

    def pads_by_scalar(lo, hi, ps):
        act(T.d[:, lo:hi], T.pad[:, :].indirect(T.ku[:, lo // 16:hi // 16]), F.Identity, 1.0, -1.0,
            [al("pad"), al("ku")], [("d", lo, hi)])

    def back(lo, hi, ps):
        act(T.sg[:, lo:hi], T[ps][:, 0:hi - lo], F.Sign, 0.5, -1.0, [al(ps)], [("sg", lo, hi)])
        act(T.n[:, lo:hi], T[ps][:, 0:hi - lo], F.Identity, 0.0, -1.0, [al(ps)], [("n", lo, hi)])
        act(T.t[:, lo:hi], T.sg[:, lo:hi], F.Identity, -128.0, -128.0, [("sg", lo, hi)], [("t", lo, hi)])

    def add_cells(lo, hi, ps):
        add_up(ps, [("I", "cel", lo, hi), ("I", "d", lo, hi)])
    pads_by_scalar(*cuts[0])
    pads_by_scalar(*cuts[1])
    add_cells(*cuts[0])
    back(*cuts[0])
    pads_by_scalar(*cuts[2])
    places(64, 1.0, 256.0, 0, lambda: fold("n", 0, XV, False))
    add_cells(*cuts[1])
    add_cells(*cuts[2])
    back(*cuts[1])
    back(*cuts[2])
    for lo, hi in ((0, DUMP), (DUMP, C)):
        scatter(0, "n", lo, hi)
    act(T.Wk[:], T.W1[:], F.Identity, 0.0, T.wk[:], [al("W1"), al("wk")], [al("Wk")])
    act(T.Z[:], T.I[:], F.Identity, 0.0, 0.0, [al("I")], [al("Z")])
    act(T.W0[:], T.W1[:], F.Identity, 0.0, T.w0[:], [al("W1"), al("w0")], [al("W0")])
    act(T.J[:], T.I[:], F.Identity, 0.0, -128.0, [al("I")], [al("J")])
    act(T.CL[:], T.pad[:, 0:CAP], F.Identity, -LIFT, 0.0, [al("pad")], [al("CL")])
    act(T.ws1[:, DUMP:], T.pad[:, 0:S], F.Silu, LIFT, 0.0, [al("pad")], [al("ws1")])
    send(0, "win0", DUMP, peers)
    fill(T.win1[:, DUMP:], 0.0, [al("win1")])
    send_keys(0, "win0", DUMP, 0)
    iota(T.ws2[:, DUMP + 768:], [[0, S - 768]], int(LIFT), 0, [("ws2", DUMP + 768, DUMP + S)])
    iota(T.win2[:, DUMP:], [[0, S]], 0, 0, [al("win2")])

    def by_vector(kn, src, slo, dst, lo, hi):
        tt(T[dst][:, lo:hi], T.pad[:, :].indirect(T[kn][:, lo // 16:hi // 16]), T[src][:, slo:slo + hi - lo], A.add,
           [al("pad"), (kn, lo // 16, hi // 16), (src, slo, slo + hi - lo)], [(dst, lo, hi)])

    halves = ((CAP, A1, "psA"), (A1, V0, "psB"))
    for h in range(1, H):
        last = h == H - 1
        st = 1.0 if last else -1.0
        src = "d" if last else "n"
        Rn, kn = "R%d" % (h - 1), "kn%d" % (h - 1)
        R = T[Rn]
        w, ws, wc = "win%d" % h, "ws%d" % h, "wc%d" % h
        own, olo = ("win0", DUMP) if h == 1 else ("wc%d" % (h - 1), 0)
        by_vector("ko%d" % (h - 1), own, olo, Rn, 0, CAP)
        add_up("psD", [("Z", "CL", 0, 96)], True, False)
        for lo, hi, ps in halves:
            add_up(ps, [("I", Rn, lo, hi)], True, False)
        mm(to_list("psD", 0, "W0", Rn, 0, V0, False, False), [al("W0"), al(Rn)], [al("psD")])
        act(T.n[:, CAP:V0], T.pad[:, :].indirect(T[kn][:, CAP // 16:V0 // 16]), F.Identity, 0.0, 1.0,
            [al("pad"), (kn, CAP // 16, V0 // 16)], [("n", CAP, V0)])
        by_vector(kn, Rn, V0, "n", V0, S)
        mm(to_list("psD", KB, "W0", "n", CAP, S, False, True), [al("W0"), ("n", CAP, S)], [al("psD")])
        fold(Rn, 0, CAP, last)
        act(T.sg[:, OV:CAP], T.t[:, OV:CAP], F.Identity, LIFT, 1.0, [("t", OV, CAP)], [("sg", OV, CAP)])
        fold("n", V0, S, last)
        tt(T.xs[:, OV:CAP], T.sg[:, OV:CAP], R[:, OV:CAP], A.subtract if last else A.add,
           [("sg", OV, CAP), (Rn, OV, CAP)], [("xs", OV, CAP)])
        if last:
            act(T.d[:, V0:S], T.n[:, V0:S], F.Identity, 0.0, -1.0, [("n", V0, S)], [("d", V0, S)])
            ts(T.d[:, 0:OV], R[:, 0:OV], -1.0, None, A.mult, None, [(Rn, 0, OV)], [("d", 0, OV)])
        for lo, hi, ps in halves:
            add_up(ps, [("I", "n", lo, hi)], False, True)
            act(T.sg[:, lo:hi], T[ps][:, 0:hi - lo], F.Sign, 0.5, 1.0, [al(ps)], [("sg", lo, hi)])

        def finish(Rn=Rn):
            for lo, hi, ps in halves:
                add_up(ps, [("I", Rn, lo, hi), ("I", "n", lo, hi), ("J", "sg", lo, hi)])
        places(96, -1.0, 255.0, KB * rank, finish)
        for (lo, hi, ps), first in zip(halves, (OV, A1)):
            act(T.xs[:, lo:hi], T[ps][:, 0:hi - lo], F.Identity, LIFT + 128.0 * st, -st, [al(ps)], [("xs", lo, hi)])
            act(T[ws][:, :].indirect(T.pu[:, first // 16:hi // 16]), T.xs[:, first:hi], F.Silu, None, None,
                [("xs", first, hi), ("pu", first // 16, hi // 16)], [al(ws)])
        for lo, hi in ((V0, V1), (V1, S), (0, OV)):
            scatter(h, Rn if lo == 0 and not last else src, lo, hi)
        b1, b2, b3 = [CAP * ((q - rank) % N) for q in far + near]
        by_pe = [(b1, b1 + F1, "psA"), (b1 + F1, b1 + CAP, "psP0"), (b2, b2 + CAP, "psP1")]
        by_act = [(b3, b3 + CAP, "psP2")] if last else [(b3 + AS, b3 + CAP, "psP2"), (0, CAP, "psP3")]
        a0, a1 = (0, CAP) if last else (b3, b3 + AS)
        for lo, hi, ps in by_pe:
            add_up(ps, [("I", "CL", 0, hi - lo)], True, False)
        for lo, hi, ps in by_pe:
            add_up(ps, [("I", w, DUMP + lo, DUMP + hi)], False, True)
        act(T.sg[:, a0:a1], T[ws][:, DUMP + a0:DUMP + a1], F.Identity, -LIFT, 1.0, [al(ws)], [("sg", a0, a1)])
        add_up("psK", [("I", w, DUMP + a0, DUMP + a1), ("I", "sg", a0, a1)])
        for i, (lo, hi, ps) in enumerate(by_act):
            act(T[ps][:, 0:hi - lo], T[ws][:, DUMP + lo:DUMP + hi], F.Identity, -LIFT, 1.0, [al(ws)], [al(ps)])
            if i == 0 and not last:
                act(T[wc][:, a0:a1], T.psK[:, 0:AS], F.Identity, 0.0, 1.0, [al("psK")], [(wc, a0, a1)])
        for i, (lo, hi, ps) in enumerate(by_pe + by_act):
            o = ws if i < len(by_pe) else w
            tt(T[wc][:, lo:hi], T[ps][:, 0:hi - lo], T[o][:, DUMP + lo:DUMP + hi], A.add, [al(ps), al(o)], [(wc, lo, hi)])
            if last and 0 < i < len(by_pe):
                send(h, wc, 0, [far[i - 1]])
            if i == len(by_pe):
                send(h, wc, 0, near if last else peers)
        if not last:
            send_keys(h, wc, 0, KB)
            keys("psB", wc, 0, CAP, 0, "ko%d" % h)

    Rl = T["R%d" % (H - 1)]

    def store(qn, q):
        lo, hi = CAP * q, CAP * (q + 1)
        return qn, op(qn, lambda: Q[qn].dma_start(T.y[:, lo:hi], T.yf[:, lo:hi]), [("yf", lo, hi)], (), sem="st%d" % q, inc=16)

    lo = CAP * rank
    act(T.yf[:, lo:lo + CAP], T.psK[:, 0:CAP], F.Relu, -1.0, 1.0, [al("psK")], [("yf", lo, lo + CAP)])
    stores = [store("s", rank)]
    for q in peers:
        count["al%d" % q] = len(lanes(q, 2))
        log.append(("Rl", CAP * q, CAP * (q + 1), True, "dma", ("al%d" % q, count["al%d" % q], {})))
    order = far + near

    def widen(qn, lo, hi):
        if qn == "v":
            ts(T.yf[:, lo:hi], Rl[:, lo:hi], -1.0, 0.0, A.add, A.max, [("Rl", lo, hi)], [("yf", lo, hi)])
        else:
            act(T.yf[:, lo:hi], Rl[:, lo:hi], F.Relu, -1.0, 1.0, [("Rl", lo, hi)], [("yf", lo, hi)])
    for q in order:
        widen("v", CAP * q, CAP * q + CAP // 2)
        widen("a", CAP * q + CAP // 2, CAP * (q + 1))
        if q != order[-1]:
            stores.append(store("s", q))
    stores.append(store("a", order[-1]))
    for qn, tok in stores:
        need(qn, tok)
    for s_, v_ in count.items():
        if waited.get(s_, 0) < v_:
            g.wait_ge(T.sem[s_], v_)
